import numpy as np
import ml_dtypes


def mxq(x, axis, fmt="e4m3"):
    dtype, down = {"e4m3": (ml_dtypes.float8_e4m3fn, 7), "e5m2": (ml_dtypes.float8_e5m2, 14)}[fmt]
    v = np.moveaxis(np.asarray(x, np.float32).astype(ml_dtypes.bfloat16).astype(np.float64), axis, -1)
    blocks = v.reshape(v.shape[:-1] + (-1, 32))
    amax = np.abs(blocks).max(-1, keepdims=True)
    byte = np.maximum(np.where(amax > 0, np.frexp(amax)[1] - 1 + 127, 0) - down, 1)
    scale = np.exp2(byte - 127.0)
    codes = (blocks / scale).astype(np.float32).astype(dtype).astype(np.float64)
    return np.moveaxis((codes * scale).reshape(v.shape), -1, axis)


WIDE = False


def mx_kscale(k):
    if not WIDE:
        return np.ones(k)
    levels = np.array([10, -10, 5, -5, 0])
    if k % 512:
        return np.exp2(np.random.permutation(np.resize(levels, k // 32))).repeat(32)
    a = np.empty((k // 512, 16))
    for p in range(k // 512):
        a[p, :8] = np.random.permutation(np.resize(levels, 8))
        for g in range(8):
            far = levels[np.abs(levels - a[p, g]) >= 10]
            a[p, g + 8] = far[np.random.randint(len(far))]
    return np.exp2(a.ravel()).repeat(32)


def f64(x):
    return np.asarray(x).astype(np.float64)


def striped(idx):
    return np.tile(idx.reshape(-1, 16).T, (8, 1)).astype(np.uint16)


def unstriped(offs):
    return offs[:16].T.reshape(-1).astype(np.int64)


E2M1 = np.array([0.0, 0.5, 1.0, 1.5, 2.0, 3.0, 4.0, 6.0, -0.0, -0.5, -1.0, -1.5, -2.0, -3.0, -4.0, -6.0])


def pack_fp4(w):
    k, n = w.shape
    w = f64(np.asarray(w, np.float32).astype(ml_dtypes.bfloat16)).reshape(k // 32, 32, n)
    amax = np.abs(w).max(1)
    mant, ex = np.frexp(amax / 6.0)
    byte = np.clip(np.where(amax > 0, np.where(mant > 0.5, ex, ex - 1) + 127, 1), 1, 254)
    scaled = (w * np.exp2(127.0 - byte)[:, None, :]).reshape(k, n).astype(np.float32)
    c = np.ascontiguousarray(scaled.reshape(k // 512, 128, 4, n).transpose(0, 1, 3, 2)).astype(ml_dtypes.float4_e2m1fn).view(np.uint8) & 0xF
    words = (c[..., 0::2] | (c[..., 1::2] << 4)).reshape(k // 512, 128, 2 * n)
    return np.ascontiguousarray(words), np.ascontiguousarray(byte.astype(np.uint8).reshape(k // 512, 16, n))


def unpack_fp4(words, scales):
    g, _, n = scales.shape
    words = np.ascontiguousarray(words).reshape(g, 128, n, 2)
    nib = np.empty((g, 128, n, 4), np.uint8)
    nib[..., 0::2] = words & 0xF
    nib[..., 1::2] = words >> 4
    vals = E2M1[nib] * np.repeat(np.exp2(scales.astype(np.float64) - 127.0), 8, axis=1)[..., None]
    return vals.transpose(0, 1, 3, 2).reshape(g * 512, n)


def planes(y):
    n, m = y.shape
    v = y.astype(np.float32).astype(ml_dtypes.bfloat16).astype(np.float64).reshape(n // 32, 32, m)
    top = np.abs(v).max(1)
    byte = np.clip(np.where(top > 0, np.frexp(top)[1] - 1 + 127 - 7, 1), 1, 254)
    codes = (v * np.exp2(127.0 - byte)[:, None, :]).reshape(n, m).astype(np.float32).astype(ml_dtypes.float8_e4m3fn).view(np.uint8)
    words = codes.reshape(n // 512, 128, 4, m).transpose(0, 1, 3, 2)
    return np.ascontiguousarray(words), np.ascontiguousarray(byte.astype(np.uint8).reshape(n // 512, 16, m))


K, T, N = 512, 512, 512


def setup_inputs():
    n = np.random.standard_normal
    s = mx_kscale(K)[:, None]
    packed_xT = pack_fp4(n((K, T)) * s)
    return {
        "x_words": packed_xT[0],
        "x_scales": packed_xT[1],
        "w1": (n((K, N)) / np.sqrt(K) / s).astype(np.float32),
        "pos1": striped(np.random.permutation(T)),
        "pos2": striped(np.random.permutation(T)),
        "pos3": striped(np.random.permutation(T)),
    }


def reference(x_words, x_scales, w1, pos1, pos2, pos3):
    xq = unpack_fp4(x_words, x_scales)
    y = mxq(f64(w1), 0, "e4m3").T @ xq
    n0 = y[:, unstriped(pos1)]
    n1 = y[:, unstriped(pos2)]
    n2 = y[:, unstriped(pos3)]
    out_0 = np.maximum(np.minimum(n0, n1), np.minimum(np.maximum(n0, n1), n2))
    return (out_0,) + planes(out_0)

@@ -1,0 +1,171 @@
+from contextlib import ExitStack
+
+import concourse.mybir as mybir
+
+K, T, N = 512, 512, 512
+FLOPS = 2 * K * T * N
+
+F32 = mybir.dt.float32
+BF16 = mybir.dt.bfloat16
+I32 = mybir.dt.int32
+U32 = mybir.dt.uint32
+U16 = mybir.dt.uint16
+U8 = mybir.dt.uint8
+FP8X4 = mybir.dt.float8_e4m3fn_x4
+FP4X4 = mybir.dt.float4_e2m1fn_x4
+MIN = mybir.AluOpType.min
+MAX = mybir.AluOpType.max
+
+P = 128
+PACK = 4
+SPARE = 192
+M_HALF = 64
+M_VECTOR = 42
+PIECES = [(0, 0, 512), (1, 0, 512), (2, 0, 512), (3, 0, 256), (3, 256, 128), (3, 384, 128)]
+
+
+def tile_picked_wmedian_none_lo_kernel(tc, x_words, x_scales, w1, pos1, pos2, pos3, out_0, out_1, out_2):
+    nc = tc.nc
+    with ExitStack() as ctx:
+        keep = ctx.enter_context(tc.tile_pool(name="keep", bufs=1))
+        psum = ctx.enter_context(tc.psum_pool(name="psum", bufs=1))
+
+        x_planes = keep.tile([P, T], U8, align_bytes=64)
+        for q in range(4):
+            nc.scalar.dma_start(
+                out=x_planes[32 * q : 32 * q + 32, :].bitcast(I32),
+                in_=x_scales[0, 4 * q : 4 * q + 4, :].bitcast(I32).unsqueeze(0).to_broadcast([8, 4, T // 4]),
+            )
+        w_rows = w1.rearrange("(p j) c -> p j c", j=PACK)
+        w_raw = []
+        for h in range(2):
+            half = keep.tile([P, PACK, N // 2], F32, name=f"w_raw{h}")
+            nc.sync.dma_start(out=half[:], in_=w_rows[:, :, h * (N // 2) : (h + 1) * (N // 2)])
+            w_raw.append(half)
+        x_codes = keep.tile([P, 2 * T], U8, align_bytes=64)
+        nc.sync.dma_start(out=x_codes[:].bitcast(I32), in_=x_words[0].bitcast(I32))
+        lists = []
+        for d, pos in enumerate((pos1, pos2, pos3)):
+            offsets = keep.tile([P, T // 16], U16, name=f"offsets{d}")
+            nc.sync.dma_start(offsets[:], pos)
+            lists.append(offsets)
+
+        y = keep.tile([P, PACK * T + SPARE], F32)
+        zeros = keep.tile([P, SPARE], F32)
+        nc.gpsimd.memset(zeros[:], 0.0)
+        nc.scalar.copy(out=y[:, PACK * T :], in_=zeros[:])
+
+        w_dealt = keep.tile([P, PACK, P, PACK], BF16, align_bytes=64)
+
+        def deal(copy, h, m0, m1):
+            copy(
+                out=w_dealt[:, :, h * M_HALF + m0 : h * M_HALF + m1, :].rearrange("p t m j -> p m t j"),
+                in_=w_raw[h][:, :, PACK * m0 : PACK * m1].rearrange("p j (m t) -> p m t j", t=PACK),
+            )
+
+        deal(nc.vector.tensor_copy, 0, 0, M_HALF)
+        deal(nc.vector.tensor_copy, 1, 0, M_VECTOR)
+        deal(nc.scalar.copy, 1, M_VECTOR, M_HALF)
+
+        w_codes = keep.tile([P, N], U32, align_bytes=64)
+        w_planes = keep.tile([P, N], U8, align_bytes=64)
+        w_flat = w_dealt[:].rearrange("p t m j -> p (t m j)")
+        for t0, t1 in ((0, 1), (1, 2), (2, 4)):
+            nc.vector.quantize_mx(
+                out=w_codes[:, t0 * P : t1 * P].bitcast(FP8X4),
+                scales=w_planes[:, t0 * P : t1 * P],
+                in_=w_flat[:, t0 * P * PACK : t1 * P * PACK],
+            )
+
+        def base(t):
+            return (PACK - 1 - t) * T
+
+        def project(t, c0, c1, copy):
+            bank = psum.tile([P, c1 - c0], F32, name=f"bank{t}_{c0}")
+            nc.tensor.matmul_mx(
+                out=bank[:],
+                lhsT=w_codes[:, t * P : (t + 1) * P].bitcast(FP8X4),
+                lhsT_scale=w_planes[:, t * P : (t + 1) * P],
+                rhs=x_codes[:, 2 * c0 : 2 * c1].bitcast(FP4X4),
+                rhs_scale=x_planes[:, c0:c1],
+                start=True,
+                stop=True,
+            )
+            copy(out=y[:, base(t) + c0 : base(t) + c1], in_=bank[:])
+
+        project(0, 0, T // 2, nc.scalar.copy)
+        project(0, T // 2, T, nc.vector.tensor_copy)
+        for t in range(1, PACK):
+            project(t, 0, T, nc.scalar.copy)
+
+        median = [keep.tile([P, 2, T], F32, name=f"median{u}") for u in range(2)]
+        rounded = keep.tile([P, T, PACK], BF16, align_bytes=64)
+        o_codes = keep.tile([P, T], U32, align_bytes=64)
+        o_planes = keep.tile([P, T], U8, align_bytes=64)
+        out_rows = out_0.rearrange("(p t) v -> p t v", t=PACK)
+        out_words = out_1[0].rearrange("p v t -> p (v t)").bitcast(I32)
+
+        work = [
+            {kind: keep.tile([P, width], F32, name=f"{kind}{i}") for kind in ("n0", "n1", "n2", "lo", "hi", "mid")}
+            for i, (t, v0, width) in enumerate(PIECES)
+        ]
+
+        def gather(i, d):
+            t, v0, width = PIECES[i]
+            window = T + SPARE if width == T else T
+            nc.vector.tensor_copy(
+                work[i][f"n{d}"][:],
+                y[:, base(t) : base(t) + window].indirect(lists[d][:, v0 // 16 : (v0 + width) // 16]),
+            )
+
+        def order_pair(i):
+            nc.vector.tensor_tensor(work[i]["lo"][:], work[i]["n0"][:], work[i]["n1"][:], MIN)
+            nc.vector.tensor_tensor(work[i]["hi"][:], work[i]["n0"][:], work[i]["n1"][:], MAX)
+
+        def cap(i):
+            nc.vector.tensor_tensor(work[i]["mid"][:], work[i]["hi"][:], work[i]["n2"][:], MIN)
+
+        def finish(i):
+            t, v0, width = PIECES[i]
+            cols = slice(v0, v0 + width)
+            nc.vector.tensor_tensor(median[t // 2][:, t % 2, cols], work[i]["lo"][:], work[i]["mid"][:], MAX)
+            nc.sync.dma_start(out=out_rows[:, t, cols], in_=median[t // 2][:, t % 2, cols])
+            if t % 2 == 1:
+                u = t // 2
+                nc.scalar.copy(
+                    out=rounded[:, cols, 2 * u : 2 * u + 2],
+                    in_=median[u][:, :, cols].rearrange("p e v -> p v e"),
+                )
+
+        def requantize(i):
+            t, v0, width = PIECES[i]
+            cols = slice(v0, v0 + width)
+            nc.vector.quantize_mx(
+                out=o_codes[:, cols].bitcast(FP8X4),
+                scales=o_planes[:, cols],
+                in_=rounded[:, cols, :].rearrange("p v t -> p (v t)"),
+            )
+            nc.sync.dma_start(out=out_words[:, cols], in_=o_codes[:, cols].bitcast(I32))
+
+        for d in range(3):
+            gather(0, d)
+        order_pair(0)
+        last = len(PIECES) - 1
+        for i in range(last):
+            gather(i + 1, 0)
+            cap(i)
+            gather(i + 1, 1)
+            finish(i)
+            gather(i + 1, 2)
+            order_pair(i + 1)
+        requantize(last - 2)
+        cap(last)
+        requantize(last - 1)
+        finish(last)
+        requantize(last)
+        for q in range(4):
+            queue = nc.sync if q % 2 == 0 else nc.scalar
+            queue.dma_start(
+                out=out_2[0, 4 * q : 4 * q + 4, :].bitcast(I32),
+                in_=o_planes[32 * q : 32 * q + 4, :].bitcast(I32),
+            )

@@ -20,8 +20,8 @@ P = 128
 PACK = 4
 SPARE = 192
 M_HALF = 64
-M_VECTOR = 42
-PIECES = [(0, 0, 512), (1, 0, 512), (2, 0, 512), (3, 0, 256), (3, 256, 128), (3, 384, 128)]
+CHUNK = 128
+STEPS = [(0, 2 * T), (2 * T, 3 * T + 2 * CHUNK), (3 * T + 2 * CHUNK, 3 * T + 3 * CHUNK), (3 * T + 3 * CHUNK, 4 * T)]
 
 
 def tile_picked_wmedian_none_lo_kernel(tc, x_words, x_scales, w1, pos1, pos2, pos3, out_0, out_1, out_2):
@@ -30,12 +30,6 @@ def tile_picked_wmedian_none_lo_kernel(tc, x_words, x_scales, w1, pos1, pos2, po
         keep = ctx.enter_context(tc.tile_pool(name="keep", bufs=1))
         psum = ctx.enter_context(tc.psum_pool(name="psum", bufs=1))
 
-        x_planes = keep.tile([P, T], U8, align_bytes=64)
-        for q in range(4):
-            nc.scalar.dma_start(
-                out=x_planes[32 * q : 32 * q + 32, :].bitcast(I32),
-                in_=x_scales[0, 4 * q : 4 * q + 4, :].bitcast(I32).unsqueeze(0).to_broadcast([8, 4, T // 4]),
-            )
         w_rows = w1.rearrange("(p j) c -> p j c", j=PACK)
         w_raw = []
         for h in range(2):
@@ -44,6 +38,12 @@ def tile_picked_wmedian_none_lo_kernel(tc, x_words, x_scales, w1, pos1, pos2, po
             w_raw.append(half)
         x_codes = keep.tile([P, 2 * T], U8, align_bytes=64)
         nc.sync.dma_start(out=x_codes[:].bitcast(I32), in_=x_words[0].bitcast(I32))
+        x_planes = keep.tile([P, T], U8, align_bytes=64)
+        for q in range(4):
+            nc.sync.dma_start(
+                out=x_planes[32 * q : 32 * q + 32, :].bitcast(I32),
+                in_=x_scales[0, 4 * q : 4 * q + 4, :].bitcast(I32).unsqueeze(0).to_broadcast([8, 4, T // 4]),
+            )
         lists = []
         for d, pos in enumerate((pos1, pos2, pos3)):
             offsets = keep.tile([P, T // 16], U16, name=f"offsets{d}")
@@ -56,26 +56,31 @@ def tile_picked_wmedian_none_lo_kernel(tc, x_words, x_scales, w1, pos1, pos2, po
         nc.scalar.copy(out=y[:, PACK * T :], in_=zeros[:])
 
         w_dealt = keep.tile([P, PACK, P, PACK], BF16, align_bytes=64)
-
-        def deal(copy, h, m0, m1):
-            copy(
-                out=w_dealt[:, :, h * M_HALF + m0 : h * M_HALF + m1, :].rearrange("p t m j -> p m t j"),
-                in_=w_raw[h][:, :, PACK * m0 : PACK * m1].rearrange("p j (m t) -> p m t j", t=PACK),
-            )
-
-        deal(nc.vector.tensor_copy, 0, 0, M_HALF)
-        deal(nc.vector.tensor_copy, 1, 0, M_VECTOR)
-        deal(nc.scalar.copy, 1, M_VECTOR, M_HALF)
-
         w_codes = keep.tile([P, N], U32, align_bytes=64)
         w_planes = keep.tile([P, N], U8, align_bytes=64)
         w_flat = w_dealt[:].rearrange("p t m j -> p (t m j)")
-        for t0, t1 in ((0, 1), (1, 2), (2, 4)):
-            nc.vector.quantize_mx(
-                out=w_codes[:, t0 * P : t1 * P].bitcast(FP8X4),
-                scales=w_planes[:, t0 * P : t1 * P],
-                in_=w_flat[:, t0 * P * PACK : t1 * P * PACK],
+
+        def deal(copy, h, t0, t1):
+            copy(
+                out=w_dealt[:, t0:t1, h * M_HALF : (h + 1) * M_HALF, :].rearrange("p t m j -> p m t j"),
+                in_=w_raw[h][:].rearrange("p j (m t) -> p m t j", t=PACK)[:, :, t0:t1, :],
             )
+
+        def quantize_w(c0, c1):
+            nc.vector.quantize_mx(
+                out=w_codes[:, c0:c1].bitcast(FP8X4),
+                scales=w_planes[:, c0:c1],
+                in_=w_flat[:, c0 * PACK : c1 * PACK],
+            )
+
+        deal(nc.vector.tensor_copy, 0, 0, PACK)
+        quantize_w(0, M_HALF)
+        deal(nc.vector.tensor_copy, 1, 0, 1)
+        deal(nc.vector.tensor_copy, 1, 1, 2)
+        deal(nc.scalar.copy, 1, 2, PACK)
+        quantize_w(M_HALF, P)
+        quantize_w(P, 2 * P)
+        quantize_w(2 * P, 4 * P)
 
         def base(t):
             return (PACK - 1 - t) * T
@@ -98,25 +103,31 @@ def tile_picked_wmedian_none_lo_kernel(tc, x_words, x_scales, w1, pos1, pos2, po
         for t in range(1, PACK):
             project(t, 0, T, nc.scalar.copy)
 
-        median = [keep.tile([P, 2, T], F32, name=f"median{u}") for u in range(2)]
+        median = keep.tile([P, PACK * T], F32)
+        median_rows = median[:].rearrange("p (t v) -> p t v", t=PACK)
         rounded = keep.tile([P, T, PACK], BF16, align_bytes=64)
         o_codes = keep.tile([P, T], U32, align_bytes=64)
         o_planes = keep.tile([P, T], U8, align_bytes=64)
-        out_rows = out_0.rearrange("(p t) v -> p t v", t=PACK)
+        out_flat = out_0.rearrange("(p t) v -> p (t v)", t=PACK)
         out_words = out_1[0].rearrange("p v t -> p (v t)").bitcast(I32)
 
         work = [
-            {kind: keep.tile([P, width], F32, name=f"{kind}{i}") for kind in ("n0", "n1", "n2", "lo", "hi", "mid")}
-            for i, (t, v0, width) in enumerate(PIECES)
+            {kind: keep.tile([P, e1 - e0], F32, name=f"{kind}{i}") for kind in ("n0", "n1", "n2", "lo", "hi", "mid")}
+            for i, (e0, e1) in enumerate(STEPS)
         ]
 
-        def gather(i, d):
-            t, v0, width = PIECES[i]
-            window = T + SPARE if width == T else T
+        def gather(i, d, t):
+            e0, e1 = STEPS[i]
+            v0, v1 = max(e0 - t * T, 0), min(e1 - t * T, T)
+            window = T + SPARE if v1 - v0 == T else T
             nc.vector.tensor_copy(
-                work[i][f"n{d}"][:],
-                y[:, base(t) : base(t) + window].indirect(lists[d][:, v0 // 16 : (v0 + width) // 16]),
+                work[i][f"n{d}"][:, t * T + v0 - e0 : t * T + v1 - e0],
+                y[:, base(t) : base(t) + window].indirect(lists[d][:, v0 // 16 : v1 // 16]),
             )
+
+        def gathers(i):
+            e0, e1 = STEPS[i]
+            return [(i, d, t) for t in range(e0 // T, (e1 - 1) // T + 1) for d in range(3)]
 
         def order_pair(i):
             nc.vector.tensor_tensor(work[i]["lo"][:], work[i]["n0"][:], work[i]["n1"][:], MIN)
@@ -126,45 +137,53 @@ def tile_picked_wmedian_none_lo_kernel(tc, x_words, x_scales, w1, pos1, pos2, po
             nc.vector.tensor_tensor(work[i]["mid"][:], work[i]["hi"][:], work[i]["n2"][:], MIN)
 
         def finish(i):
-            t, v0, width = PIECES[i]
-            cols = slice(v0, v0 + width)
-            nc.vector.tensor_tensor(median[t // 2][:, t % 2, cols], work[i]["lo"][:], work[i]["mid"][:], MAX)
-            nc.sync.dma_start(out=out_rows[:, t, cols], in_=median[t // 2][:, t % 2, cols])
-            if t % 2 == 1:
-                u = t // 2
-                nc.scalar.copy(
-                    out=rounded[:, cols, 2 * u : 2 * u + 2],
-                    in_=median[u][:, :, cols].rearrange("p e v -> p v e"),
-                )
+            e0, e1 = STEPS[i]
+            nc.vector.tensor_tensor(median[:, e0:e1], work[i]["lo"][:], work[i]["mid"][:], MAX)
+            nc.sync.dma_start(out=out_flat[:, e0:e1], in_=median[:, e0:e1])
 
-        def requantize(i):
-            t, v0, width = PIECES[i]
-            cols = slice(v0, v0 + width)
+        def round_pair(copy, u, v0, v1):
+            copy(
+                out=rounded[:, v0:v1, 2 * u : 2 * u + 2],
+                in_=median_rows[:, 2 * u : 2 * u + 2, v0:v1].rearrange("p e v -> p v e"),
+            )
+
+        def requantize(c):
+            cols = slice(c * CHUNK, (c + 1) * CHUNK)
             nc.vector.quantize_mx(
                 out=o_codes[:, cols].bitcast(FP8X4),
                 scales=o_planes[:, cols],
                 in_=rounded[:, cols, :].rearrange("p v t -> p (v t)"),
             )
-            nc.sync.dma_start(out=out_words[:, cols], in_=o_codes[:, cols].bitcast(I32))
 
-        for d in range(3):
-            gather(0, d)
+        def store_words(v0, v1):
+            nc.sync.dma_start(out=out_words[:, v0:v1], in_=o_codes[:, v0:v1].bitcast(I32))
+
+        for args in gathers(0):
+            gather(*args)
         order_pair(0)
-        last = len(PIECES) - 1
+        ready = [(0, 0, T), (1, 0, 2 * CHUNK), (1, 2 * CHUNK, 3 * CHUNK)]
+        last = len(STEPS) - 1
         for i in range(last):
-            gather(i + 1, 0)
+            ahead = gathers(i + 1)
+            gather(*ahead[0])
             cap(i)
-            gather(i + 1, 1)
+            gather(*ahead[1])
             finish(i)
-            gather(i + 1, 2)
+            round_pair(nc.scalar.copy, *ready[i])
+            for args in ahead[2:]:
+                gather(*args)
             order_pair(i + 1)
-        requantize(last - 2)
+        requantize(0)
         cap(last)
-        requantize(last - 1)
+        requantize(1)
         finish(last)
-        requantize(last)
+        requantize(2)
+        store_words(0, 3 * CHUNK)
+        round_pair(nc.vector.tensor_copy, 1, 3 * CHUNK, T)
+        requantize(3)
+        store_words(3 * CHUNK, T)
         for q in range(4):
-            queue = nc.sync if q % 2 == 0 else nc.scalar
+            queue = nc.scalar if q % 2 == 0 else nc.sync
             queue.dma_start(
                 out=out_2[0, 4 * q : 4 * q + 4, :].bitcast(I32),
                 in_=o_planes[32 * q : 32 * q + 4, :].bitcast(I32),

@@ -21,7 +21,7 @@ PACK = 4
 SPARE = 192
 M_HALF = 64
 CHUNK = 128
-STEPS = [(0, 2 * T), (2 * T, 3 * T + 2 * CHUNK), (3 * T + 2 * CHUNK, 3 * T + 3 * CHUNK), (3 * T + 3 * CHUNK, 4 * T)]
+STEPS = [(0, T), (T, 2 * T), (2 * T, 3 * T + 2 * CHUNK), (3 * T + 2 * CHUNK, 3 * T + 3 * CHUNK), (3 * T + 3 * CHUNK, 4 * T)]
 
 
 def tile_picked_wmedian_none_lo_kernel(tc, x_words, x_scales, w1, pos1, pos2, pos3, out_0, out_1, out_2):
@@ -31,56 +31,47 @@ def tile_picked_wmedian_none_lo_kernel(tc, x_words, x_scales, w1, pos1, pos2, po
         psum = ctx.enter_context(tc.psum_pool(name="psum", bufs=1))
 
         w_rows = w1.rearrange("(p j) c -> p j c", j=PACK)
-        w_raw = []
-        for h in range(2):
-            half = keep.tile([P, PACK, N // 2], F32, name=f"w_raw{h}")
-            nc.sync.dma_start(out=half[:], in_=w_rows[:, :, h * (N // 2) : (h + 1) * (N // 2)])
-            w_raw.append(half)
+        w_raw = [keep.tile([P, PACK, N // 2], F32, name=f"w_raw{h}") for h in range(2)]
+        lists = [keep.tile([P, T // 16], U16, name=f"offsets{d}") for d in range(3)]
         x_codes = keep.tile([P, 2 * T], U8, align_bytes=64)
-        nc.sync.dma_start(out=x_codes[:].bitcast(I32), in_=x_words[0].bitcast(I32))
         x_planes = keep.tile([P, T], U8, align_bytes=64)
+
+        for u in range(2):
+            nc.sync.dma_start(out=w_raw[0][:, 2 * u : 2 * u + 2, :], in_=w_rows[:, 2 * u : 2 * u + 2, : N // 2])
+        nc.sync.dma_start(out=x_codes[:].bitcast(I32), in_=x_words[0].bitcast(I32))
         for q in range(4):
             nc.sync.dma_start(
                 out=x_planes[32 * q : 32 * q + 32, :].bitcast(I32),
                 in_=x_scales[0, 4 * q : 4 * q + 4, :].bitcast(I32).unsqueeze(0).to_broadcast([8, 4, T // 4]),
             )
-        lists = []
-        for d, pos in enumerate((pos1, pos2, pos3)):
-            offsets = keep.tile([P, T // 16], U16, name=f"offsets{d}")
-            nc.sync.dma_start(offsets[:], pos)
-            lists.append(offsets)
+        nc.sync.dma_start(lists[0][:], pos1)
+        nc.sync.dma_start(out=w_raw[1][:], in_=w_rows[:, :, N // 2 :])
+        nc.sync.dma_start(lists[1][:], pos2)
+        nc.sync.dma_start(lists[2][:], pos3)
 
         y = keep.tile([P, PACK * T + SPARE], F32)
         zeros = keep.tile([P, SPARE], F32)
         nc.gpsimd.memset(zeros[:], 0.0)
         nc.scalar.copy(out=y[:, PACK * T :], in_=zeros[:])
 
-        w_dealt = keep.tile([P, PACK, P, PACK], BF16, align_bytes=64)
+        dealt_a = keep.tile([P, 2, M_HALF, PACK], BF16, align_bytes=64)
+        dealt_b = keep.tile([P, 2, M_HALF, PACK], BF16, align_bytes=64, tag="shared")
+        dealt_cd = keep.tile([P, 2, P, PACK], BF16, align_bytes=64)
         w_codes = keep.tile([P, N], U32, align_bytes=64)
         w_planes = keep.tile([P, N], U8, align_bytes=64)
-        w_flat = w_dealt[:].rearrange("p t m j -> p (t m j)")
 
-        def deal(copy, h, t0, t1):
+        def deal(copy, dst, h, t0, j0=0, j1=PACK):
             copy(
-                out=w_dealt[:, t0:t1, h * M_HALF : (h + 1) * M_HALF, :].rearrange("p t m j -> p m t j"),
-                in_=w_raw[h][:].rearrange("p j (m t) -> p m t j", t=PACK)[:, :, t0:t1, :],
+                out=dst.rearrange("p t m j -> p m t j")[:, :, :, j0:j1],
+                in_=w_raw[h][:].rearrange("p j (m t) -> p m t j", t=PACK)[:, :, t0 : t0 + 2, j0:j1],
             )
 
-        def quantize_w(c0, c1):
+        def quantize_w(src, c0, c1):
             nc.vector.quantize_mx(
                 out=w_codes[:, c0:c1].bitcast(FP8X4),
                 scales=w_planes[:, c0:c1],
-                in_=w_flat[:, c0 * PACK : c1 * PACK],
+                in_=src[:].rearrange("p t m j -> p (t m j)"),
             )
-
-        deal(nc.vector.tensor_copy, 0, 0, PACK)
-        quantize_w(0, M_HALF)
-        deal(nc.vector.tensor_copy, 1, 0, 1)
-        deal(nc.vector.tensor_copy, 1, 1, 2)
-        deal(nc.scalar.copy, 1, 2, PACK)
-        quantize_w(M_HALF, P)
-        quantize_w(P, 2 * P)
-        quantize_w(2 * P, 4 * P)
 
         def base(t):
             return (PACK - 1 - t) * T
@@ -98,30 +89,41 @@ def tile_picked_wmedian_none_lo_kernel(tc, x_words, x_scales, w1, pos1, pos2, po
             )
             copy(out=y[:, base(t) + c0 : base(t) + c1], in_=bank[:])
 
-        project(0, 0, T // 2, nc.scalar.copy)
-        project(0, T // 2, T, nc.vector.tensor_copy)
-        for t in range(1, PACK):
-            project(t, 0, T, nc.scalar.copy)
+        deal(nc.vector.tensor_copy, dealt_a[:], 0, 0, 0, 2)
+        deal(nc.vector.tensor_copy, dealt_a[:], 0, 0, 2, 4)
+        quantize_w(dealt_a, 0, P)
+        deal(nc.scalar.copy, dealt_cd[:, :, :M_HALF, :], 0, 2)
+        for c in range(T // CHUNK):
+            project(0, c * CHUNK, (c + 1) * CHUNK, nc.vector.tensor_copy)
+        deal(nc.scalar.copy, dealt_b[:], 1, 0)
+        deal(nc.scalar.copy, dealt_cd[:, :, M_HALF:, :], 1, 2)
 
-        median = keep.tile([P, PACK * T], F32)
-        median_rows = median[:].rearrange("p (t v) -> p t v", t=PACK)
+        front = keep.tile([P, 3, T], F32)
+        back = keep.tile([P, 2 * T], F32)
+        back_rows = back[:].rearrange("p (t v) -> p t v", t=2)
         rounded = keep.tile([P, T, PACK], BF16, align_bytes=64)
         o_codes = keep.tile([P, T], U32, align_bytes=64)
         o_planes = keep.tile([P, T], U8, align_bytes=64)
         out_flat = out_0.rearrange("(p t) v -> p (t v)", t=PACK)
         out_words = out_1[0].rearrange("p v t -> p (v t)").bitcast(I32)
 
-        work = [
-            {kind: keep.tile([P, e1 - e0], F32, name=f"{kind}{i}") for kind in ("n0", "n1", "n2", "lo", "hi", "mid")}
-            for i, (e0, e1) in enumerate(STEPS)
-        ]
+        work = {}
+
+        def scratch(i, kind):
+            if (i, kind) not in work:
+                e0, e1 = STEPS[i]
+                if (i, kind) == (0, "hi"):
+                    work[(i, kind)] = keep.tile([P, e1 - e0], F32, name="hi0", align_bytes=64, tag="shared")
+                else:
+                    work[(i, kind)] = keep.tile([P, e1 - e0], F32, name=f"{kind}{i}")
+            return work[(i, kind)]
 
         def gather(i, d, t):
             e0, e1 = STEPS[i]
             v0, v1 = max(e0 - t * T, 0), min(e1 - t * T, T)
             window = T + SPARE if v1 - v0 == T else T
             nc.vector.tensor_copy(
-                work[i][f"n{d}"][:, t * T + v0 - e0 : t * T + v1 - e0],
+                scratch(i, f"n{d}")[:, t * T + v0 - e0 : t * T + v1 - e0],
                 y[:, base(t) : base(t) + window].indirect(lists[d][:, v0 // 16 : v1 // 16]),
             )
 
@@ -130,22 +132,28 @@ def tile_picked_wmedian_none_lo_kernel(tc, x_words, x_scales, w1, pos1, pos2, po
             return [(i, d, t) for t in range(e0 // T, (e1 - 1) // T + 1) for d in range(3)]
 
         def order_pair(i):
-            nc.vector.tensor_tensor(work[i]["lo"][:], work[i]["n0"][:], work[i]["n1"][:], MIN)
-            nc.vector.tensor_tensor(work[i]["hi"][:], work[i]["n0"][:], work[i]["n1"][:], MAX)
+            nc.vector.tensor_tensor(scratch(i, "hi")[:], scratch(i, "n0")[:], scratch(i, "n1")[:], MAX)
+            nc.vector.tensor_tensor(scratch(i, "lo")[:], scratch(i, "n0")[:], scratch(i, "n1")[:], MIN)
 
         def cap(i):
-            nc.vector.tensor_tensor(work[i]["mid"][:], work[i]["hi"][:], work[i]["n2"][:], MIN)
+            nc.vector.tensor_tensor(scratch(i, "mid")[:], scratch(i, "hi")[:], scratch(i, "n2")[:], MIN)
 
         def finish(i):
             e0, e1 = STEPS[i]
-            nc.vector.tensor_tensor(median[:, e0:e1], work[i]["lo"][:], work[i]["mid"][:], MAX)
-            nc.sync.dma_start(out=out_flat[:, e0:e1], in_=median[:, e0:e1])
+            dst = front[:, 2 * i, :] if i < 2 else back[:, e0 - 2 * T : e1 - 2 * T]
+            nc.vector.tensor_tensor(dst, scratch(i, "lo")[:], scratch(i, "mid")[:], MAX)
+            if i >= 2:
+                nc.sync.dma_start(out=out_flat[:, e0:e1], in_=dst)
 
-        def round_pair(copy, u, v0, v1):
-            copy(
-                out=rounded[:, v0:v1, 2 * u : 2 * u + 2],
-                in_=median_rows[:, 2 * u : 2 * u + 2, v0:v1].rearrange("p e v -> p v e"),
-            )
+        def swap(h):
+            rows = slice(h * M_HALF, (h + 1) * M_HALF)
+            other = slice((1 - h) * M_HALF, (2 - h) * M_HALF)
+            nc.sync.dma_start(out=front[rows, 1, :], in_=front[other, 2 * h, :])
+            nc.sync.dma_start(out=out_flat[rows, : 2 * T], in_=front[rows, h : h + 2, :].rearrange("p t v -> p (t v)"))
+            nc.scalar.copy(out=rounded[rows, :, 0:2], in_=front[rows, h : h + 2, :].rearrange("p e v -> p v e"))
+
+        def round_back(copy, v0, v1):
+            copy(out=rounded[:, v0:v1, 2:4], in_=back_rows[:, :, v0:v1].rearrange("p e v -> p v e"))
 
         def requantize(c):
             cols = slice(c * CHUNK, (c + 1) * CHUNK)
@@ -160,17 +168,31 @@ def tile_picked_wmedian_none_lo_kernel(tc, x_words, x_scales, w1, pos1, pos2, po
 
         for args in gathers(0):
             gather(*args)
+        quantize_w(dealt_b, P, 2 * P)
+        project(1, 0, T, nc.scalar.copy)
         order_pair(0)
-        ready = [(0, 0, T), (1, 0, 2 * CHUNK), (1, 2 * CHUNK, 3 * CHUNK)]
+        cap(0)
+        quantize_w(dealt_cd, 2 * P, 4 * P)
+        project(2, 0, T, nc.scalar.copy)
+        project(3, 0, T, nc.scalar.copy)
+        finish(0)
+        swap(0)
+        for args in gathers(1):
+            gather(*args)
+        order_pair(1)
         last = len(STEPS) - 1
-        for i in range(last):
+        for i in range(1, last):
             ahead = gathers(i + 1)
-            gather(*ahead[0])
             cap(i)
-            gather(*ahead[1])
+            gather(*ahead[0])
             finish(i)
-            round_pair(nc.scalar.copy, *ready[i])
-            for args in ahead[2:]:
+            if i == 1:
+                swap(1)
+            elif i == 2:
+                round_back(nc.scalar.copy, 0, 2 * CHUNK)
+            else:
+                round_back(nc.scalar.copy, 2 * CHUNK, 3 * CHUNK)
+            for args in ahead[1:]:
                 gather(*args)
             order_pair(i + 1)
         requantize(0)
@@ -179,7 +201,7 @@ def tile_picked_wmedian_none_lo_kernel(tc, x_words, x_scales, w1, pos1, pos2, po
         finish(last)
         requantize(2)
         store_words(0, 3 * CHUNK)
-        round_pair(nc.vector.tensor_copy, 1, 3 * CHUNK, T)
+        round_back(nc.vector.tensor_copy, 3 * CHUNK, T)
         requantize(3)
         store_words(3 * CHUNK, T)
         for q in range(4):

@@ -36,14 +36,15 @@ def tile_picked_wmedian_none_lo_kernel(tc, x_words, x_scales, w1, pos1, pos2, po
         x_codes = keep.tile([P, 2 * T], U8, align_bytes=64)
         x_planes = keep.tile([P, T], U8, align_bytes=64)
 
+        nc.vector.memset(x_planes[:].bitcast(I32), 0)
         for u in range(2):
             nc.sync.dma_start(out=w_raw[0][:, 2 * u : 2 * u + 2, :], in_=w_rows[:, 2 * u : 2 * u + 2, : N // 2])
-        nc.sync.dma_start(out=x_codes[:].bitcast(I32), in_=x_words[0].bitcast(I32))
         for q in range(4):
             nc.sync.dma_start(
-                out=x_planes[32 * q : 32 * q + 32, :].bitcast(I32),
-                in_=x_scales[0, 4 * q : 4 * q + 4, :].bitcast(I32).unsqueeze(0).to_broadcast([8, 4, T // 4]),
+                out=x_planes[32 * q : 32 * q + 4, :].bitcast(I32),
+                in_=x_scales[0, 4 * q : 4 * q + 4, :].bitcast(I32),
             )
+        nc.sync.dma_start(out=x_codes[:].bitcast(I32), in_=x_words[0].bitcast(I32))
         nc.sync.dma_start(lists[0][:], pos1)
         nc.sync.dma_start(out=w_raw[1][:], in_=w_rows[:, :, N // 2 :])
         nc.sync.dma_start(lists[1][:], pos2)
@@ -56,22 +57,27 @@ def tile_picked_wmedian_none_lo_kernel(tc, x_words, x_scales, w1, pos1, pos2, po
 
         dealt_a = keep.tile([P, 2, M_HALF, PACK], BF16, align_bytes=64)
         dealt_b = keep.tile([P, 2, M_HALF, PACK], BF16, align_bytes=64, tag="shared")
-        dealt_cd = keep.tile([P, 2, P, PACK], BF16, align_bytes=64)
+        dealt_cd = [keep.tile([P, 2, M_HALF, PACK], BF16, align_bytes=64, name=f"dealt_cd{h}") for h in range(2)]
         w_codes = keep.tile([P, N], U32, align_bytes=64)
         w_planes = keep.tile([P, N], U8, align_bytes=64)
 
-        def deal(copy, dst, h, t0, j0=0, j1=PACK):
+        def deal(copy, dst, h, t0, j0=0, j1=PACK, slots=2):
             copy(
                 out=dst.rearrange("p t m j -> p m t j")[:, :, :, j0:j1],
-                in_=w_raw[h][:].rearrange("p j (m t) -> p m t j", t=PACK)[:, :, t0 : t0 + 2, j0:j1],
+                in_=w_raw[h][:].rearrange("p j (m t) -> p m t j", t=PACK)[:, :, t0 : t0 + slots, j0:j1],
             )
 
         def quantize_w(src, c0, c1):
             nc.vector.quantize_mx(
                 out=w_codes[:, c0:c1].bitcast(FP8X4),
                 scales=w_planes[:, c0:c1],
-                in_=src[:].rearrange("p t m j -> p (t m j)"),
+                in_=src.rearrange("p t m j -> p (t m j)"),
             )
+
+        def quantize_cd(h):
+            for t in range(2):
+                c0 = (2 + t) * P + h * M_HALF
+                quantize_w(dealt_cd[h][:, t : t + 1], c0, c0 + M_HALF)
 
         def base(t):
             return (PACK - 1 - t) * T
@@ -90,13 +96,16 @@ def tile_picked_wmedian_none_lo_kernel(tc, x_words, x_scales, w1, pos1, pos2, po
             copy(out=y[:, base(t) + c0 : base(t) + c1], in_=bank[:])
 
         deal(nc.vector.tensor_copy, dealt_a[:], 0, 0, 0, 2)
-        deal(nc.vector.tensor_copy, dealt_a[:], 0, 0, 2, 4)
-        quantize_w(dealt_a, 0, P)
-        deal(nc.scalar.copy, dealt_cd[:, :, :M_HALF, :], 0, 2)
+        for t in range(2):
+            deal(nc.vector.tensor_copy, dealt_a[:, t : t + 1], 0, t, 2, 4, 1)
+        for t in range(2):
+            quantize_w(dealt_a[:, t : t + 1], t * M_HALF, (t + 1) * M_HALF)
+        deal(nc.scalar.copy, dealt_cd[0][:], 0, 2)
+        quantize_cd(0)
         for c in range(T // CHUNK):
             project(0, c * CHUNK, (c + 1) * CHUNK, nc.vector.tensor_copy)
         deal(nc.scalar.copy, dealt_b[:], 1, 0)
-        deal(nc.scalar.copy, dealt_cd[:, :, M_HALF:, :], 1, 2)
+        deal(nc.scalar.copy, dealt_cd[1][:], 1, 2)
 
         front = keep.tile([P, 3, T], F32)
         back = keep.tile([P, 2 * T], F32)
@@ -112,10 +121,13 @@ def tile_picked_wmedian_none_lo_kernel(tc, x_words, x_scales, w1, pos1, pos2, po
         def scratch(i, kind):
             if (i, kind) not in work:
                 e0, e1 = STEPS[i]
-                if (i, kind) == (0, "hi"):
-                    work[(i, kind)] = keep.tile([P, e1 - e0], F32, name="hi0", align_bytes=64, tag="shared")
+                if i == 0 and kind in ("n2", "hi", "lo"):
+                    late = keep.tile([P, 3, T], F32, name="late", align_bytes=64, tag="shared")
+                    for row, name in enumerate(("n2", "hi", "lo")):
+                        work[(0, name)] = late[:, row, :]
                 else:
-                    work[(i, kind)] = keep.tile([P, e1 - e0], F32, name=f"{kind}{i}")
+                    whole = keep.tile([P, e1 - e0], F32, name=f"{kind}{i}")
+                    work[(i, kind)] = whole[:]
             return work[(i, kind)]
 
         def gather(i, d, t):
@@ -132,16 +144,16 @@ def tile_picked_wmedian_none_lo_kernel(tc, x_words, x_scales, w1, pos1, pos2, po
             return [(i, d, t) for t in range(e0 // T, (e1 - 1) // T + 1) for d in range(3)]
 
         def order_pair(i):
-            nc.vector.tensor_tensor(scratch(i, "hi")[:], scratch(i, "n0")[:], scratch(i, "n1")[:], MAX)
-            nc.vector.tensor_tensor(scratch(i, "lo")[:], scratch(i, "n0")[:], scratch(i, "n1")[:], MIN)
+            nc.vector.tensor_tensor(scratch(i, "hi"), scratch(i, "n0"), scratch(i, "n1"), MAX)
+            nc.vector.tensor_tensor(scratch(i, "lo"), scratch(i, "n0"), scratch(i, "n1"), MIN)
 
         def cap(i):
-            nc.vector.tensor_tensor(scratch(i, "mid")[:], scratch(i, "hi")[:], scratch(i, "n2")[:], MIN)
+            nc.vector.tensor_tensor(scratch(i, "mid"), scratch(i, "hi"), scratch(i, "n2"), MIN)
 
         def finish(i):
             e0, e1 = STEPS[i]
             dst = front[:, 2 * i, :] if i < 2 else back[:, e0 - 2 * T : e1 - 2 * T]
-            nc.vector.tensor_tensor(dst, scratch(i, "lo")[:], scratch(i, "mid")[:], MAX)
+            nc.vector.tensor_tensor(dst, scratch(i, "lo"), scratch(i, "mid"), MAX)
             if i >= 2:
                 nc.sync.dma_start(out=out_flat[:, e0:e1], in_=dst)
 
@@ -166,13 +178,14 @@ def tile_picked_wmedian_none_lo_kernel(tc, x_words, x_scales, w1, pos1, pos2, po
         def store_words(v0, v1):
             nc.sync.dma_start(out=out_words[:, v0:v1], in_=o_codes[:, v0:v1].bitcast(I32))
 
-        for args in gathers(0):
-            gather(*args)
-        quantize_w(dealt_b, P, 2 * P)
+        gather(0, 0, 0)
+        gather(0, 1, 0)
+        quantize_w(dealt_b[:], P, 2 * P)
         project(1, 0, T, nc.scalar.copy)
+        gather(0, 2, 0)
         order_pair(0)
         cap(0)
-        quantize_w(dealt_cd, 2 * P, 4 * P)
+        quantize_cd(1)
         project(2, 0, T, nc.scalar.copy)
         project(3, 0, T, nc.scalar.copy)
         finish(0)
@@ -195,13 +208,13 @@ def tile_picked_wmedian_none_lo_kernel(tc, x_words, x_scales, w1, pos1, pos2, po
             for args in ahead[1:]:
                 gather(*args)
             order_pair(i + 1)
-        requantize(0)
         cap(last)
-        requantize(1)
+        requantize(0)
         finish(last)
+        requantize(1)
+        round_back(nc.vector.tensor_copy, 3 * CHUNK, T)
         requantize(2)
         store_words(0, 3 * CHUNK)
-        round_back(nc.vector.tensor_copy, 3 * CHUNK, T)
         requantize(3)
         store_words(3 * CHUNK, T)
         for q in range(4):

@@ -18,7 +18,7 @@ MAX = mybir.AluOpType.max
 
 P = 128
 PACK = 4
-SPARE = 192
+SPARE = 176
 M_HALF = 64
 CHUNK = 128
 STEPS = [(0, T), (T, 2 * T), (2 * T, 3 * T + 2 * CHUNK), (3 * T + 2 * CHUNK, 3 * T + 3 * CHUNK), (3 * T + 3 * CHUNK, 4 * T)]
@@ -40,7 +40,7 @@ def tile_picked_wmedian_none_lo_kernel(tc, x_words, x_scales, w1, pos1, pos2, po
         for u in range(2):
             nc.sync.dma_start(out=w_raw[0][:, 2 * u : 2 * u + 2, :], in_=w_rows[:, 2 * u : 2 * u + 2, : N // 2])
         for q in range(4):
-            nc.sync.dma_start(
+            nc.scalar.dma_start(
                 out=x_planes[32 * q : 32 * q + 4, :].bitcast(I32),
                 in_=x_scales[0, 4 * q : 4 * q + 4, :].bitcast(I32),
             )
@@ -52,7 +52,7 @@ def tile_picked_wmedian_none_lo_kernel(tc, x_words, x_scales, w1, pos1, pos2, po
 
         y = keep.tile([P, PACK * T + SPARE], F32)
         zeros = keep.tile([P, SPARE], F32)
-        nc.gpsimd.memset(zeros[:], 0.0)
+        nc.vector.memset(zeros[:], 0.0)
         nc.scalar.copy(out=y[:, PACK * T :], in_=zeros[:])
 
         dealt_a = keep.tile([P, 2, M_HALF, PACK], BF16, align_bytes=64)
@@ -96,11 +96,12 @@ def tile_picked_wmedian_none_lo_kernel(tc, x_words, x_scales, w1, pos1, pos2, po
             copy(out=y[:, base(t) + c0 : base(t) + c1], in_=bank[:])
 
         deal(nc.vector.tensor_copy, dealt_a[:], 0, 0, 0, 2)
+        deal(nc.vector.tensor_copy, dealt_cd[0][:], 0, 2, 0, 2)
         for t in range(2):
             deal(nc.vector.tensor_copy, dealt_a[:, t : t + 1], 0, t, 2, 4, 1)
         for t in range(2):
             quantize_w(dealt_a[:, t : t + 1], t * M_HALF, (t + 1) * M_HALF)
-        deal(nc.scalar.copy, dealt_cd[0][:], 0, 2)
+        deal(nc.scalar.copy, dealt_cd[0][:], 0, 2, 2, 4)
         quantize_cd(0)
         for c in range(T // CHUNK):
             project(0, c * CHUNK, (c + 1) * CHUNK, nc.vector.tensor_copy)
@@ -143,9 +144,15 @@ def tile_picked_wmedian_none_lo_kernel(tc, x_words, x_scales, w1, pos1, pos2, po
             e0, e1 = STEPS[i]
             return [(i, d, t) for t in range(e0 // T, (e1 - 1) // T + 1) for d in range(3)]
 
-        def order_pair(i):
+        def upper(i):
             nc.vector.tensor_tensor(scratch(i, "hi"), scratch(i, "n0"), scratch(i, "n1"), MAX)
+
+        def lower(i):
             nc.vector.tensor_tensor(scratch(i, "lo"), scratch(i, "n0"), scratch(i, "n1"), MIN)
+
+        def order_pair(i):
+            upper(i)
+            lower(i)
 
         def cap(i):
             nc.vector.tensor_tensor(scratch(i, "mid"), scratch(i, "hi"), scratch(i, "n2"), MIN)
@@ -193,21 +200,31 @@ def tile_picked_wmedian_none_lo_kernel(tc, x_words, x_scales, w1, pos1, pos2, po
         for args in gathers(1):
             gather(*args)
         order_pair(1)
-        last = len(STEPS) - 1
-        for i in range(1, last):
-            ahead = gathers(i + 1)
-            cap(i)
-            gather(*ahead[0])
-            finish(i)
-            if i == 1:
-                swap(1)
-            elif i == 2:
-                round_back(nc.scalar.copy, 0, 2 * CHUNK)
-            else:
-                round_back(nc.scalar.copy, 2 * CHUNK, 3 * CHUNK)
-            for args in ahead[1:]:
-                gather(*args)
-            order_pair(i + 1)
+        ahead = gathers(2)
+        cap(1)
+        gather(*ahead[0])
+        finish(1)
+        swap(1)
+        for args in ahead[1:]:
+            gather(*args)
+        order_pair(2)
+        gather(3, 0, 3)
+        cap(2)
+        gather(3, 1, 3)
+        finish(2)
+        round_back(nc.scalar.copy, 0, 2 * CHUNK)
+        upper(3)
+        gather(3, 2, 3)
+        gather(4, 0, 3)
+        gather(4, 1, 3)
+        lower(3)
+        cap(3)
+        upper(4)
+        gather(4, 2, 3)
+        finish(3)
+        round_back(nc.scalar.copy, 2 * CHUNK, 3 * CHUNK)
+        lower(4)
+        last = 4
         cap(last)
         requantize(0)
         finish(last)

@@ -161,7 +161,7 @@ def tile_picked_wmedian_none_lo_kernel(tc, x_words, x_scales, w1, pos1, pos2, po
             e0, e1 = STEPS[i]
             dst = front[:, 2 * i, :] if i < 2 else back[:, e0 - 2 * T : e1 - 2 * T]
             nc.vector.tensor_tensor(dst, scratch(i, "lo"), scratch(i, "mid"), MAX)
-            if i >= 2:
+            if i == 2:
                 nc.sync.dma_start(out=out_flat[:, e0:e1], in_=dst)
 
         def swap(h):
@@ -182,8 +182,8 @@ def tile_picked_wmedian_none_lo_kernel(tc, x_words, x_scales, w1, pos1, pos2, po
                 in_=rounded[:, cols, :].rearrange("p v t -> p (v t)"),
             )
 
-        def store_words(v0, v1):
-            nc.sync.dma_start(out=out_words[:, v0:v1], in_=o_codes[:, v0:v1].bitcast(I32))
+        def store_words(v0, v1, queue=nc.sync):
+            queue.dma_start(out=out_words[:, v0:v1], in_=o_codes[:, v0:v1].bitcast(I32))
 
         gather(0, 0, 0)
         gather(0, 1, 0)
@@ -228,10 +228,12 @@ def tile_picked_wmedian_none_lo_kernel(tc, x_words, x_scales, w1, pos1, pos2, po
         cap(last)
         requantize(0)
         finish(last)
+        nc.sync.dma_start(out=out_flat[:, STEPS[3][0] :], in_=back[:, STEPS[3][0] - 2 * T :])
         requantize(1)
+        store_words(0, 2 * CHUNK)
         round_back(nc.vector.tensor_copy, 3 * CHUNK, T)
         requantize(2)
-        store_words(0, 3 * CHUNK)
+        store_words(2 * CHUNK, 3 * CHUNK, nc.scalar)
         requantize(3)
         store_words(3 * CHUNK, T)
         for q in range(4):

@@ -36,15 +36,15 @@ def tile_picked_wmedian_none_lo_kernel(tc, x_words, x_scales, w1, pos1, pos2, po
         x_codes = keep.tile([P, 2 * T], U8, align_bytes=64)
         x_planes = keep.tile([P, T], U8, align_bytes=64)
 
-        nc.vector.memset(x_planes[:].bitcast(I32), 0)
         for u in range(2):
             nc.sync.dma_start(out=w_raw[0][:, 2 * u : 2 * u + 2, :], in_=w_rows[:, 2 * u : 2 * u + 2, : N // 2])
+        nc.sync.dma_start(out=x_codes[:].bitcast(I32), in_=x_words[0].bitcast(I32))
         for q in range(4):
-            nc.scalar.dma_start(
+            queue = nc.scalar if q < 2 else nc.sync
+            queue.dma_start(
                 out=x_planes[32 * q : 32 * q + 4, :].bitcast(I32),
                 in_=x_scales[0, 4 * q : 4 * q + 4, :].bitcast(I32),
             )
-        nc.sync.dma_start(out=x_codes[:].bitcast(I32), in_=x_words[0].bitcast(I32))
         nc.sync.dma_start(lists[0][:], pos1)
         nc.sync.dma_start(out=w_raw[1][:], in_=w_rows[:, :, N // 2 :])
         nc.sync.dma_start(lists[1][:], pos2)

@@ -161,7 +161,7 @@ def tile_picked_wmedian_none_lo_kernel(tc, x_words, x_scales, w1, pos1, pos2, po
             e0, e1 = STEPS[i]
             dst = front[:, 2 * i, :] if i < 2 else back[:, e0 - 2 * T : e1 - 2 * T]
             nc.vector.tensor_tensor(dst, scratch(i, "lo"), scratch(i, "mid"), MAX)
-            if i == 2:
+            if i >= 2:
                 nc.sync.dma_start(out=out_flat[:, e0:e1], in_=dst)
 
         def swap(h):
@@ -182,8 +182,8 @@ def tile_picked_wmedian_none_lo_kernel(tc, x_words, x_scales, w1, pos1, pos2, po
                 in_=rounded[:, cols, :].rearrange("p v t -> p (v t)"),
             )
 
-        def store_words(v0, v1, queue=nc.sync):
-            queue.dma_start(out=out_words[:, v0:v1], in_=o_codes[:, v0:v1].bitcast(I32))
+        def store_words(v0, v1):
+            nc.sync.dma_start(out=out_words[:, v0:v1], in_=o_codes[:, v0:v1].bitcast(I32))
 
         gather(0, 0, 0)
         gather(0, 1, 0)
@@ -228,16 +228,14 @@ def tile_picked_wmedian_none_lo_kernel(tc, x_words, x_scales, w1, pos1, pos2, po
         cap(last)
         requantize(0)
         finish(last)
-        nc.sync.dma_start(out=out_flat[:, STEPS[3][0] :], in_=back[:, STEPS[3][0] - 2 * T :])
         requantize(1)
-        store_words(0, 2 * CHUNK)
         round_back(nc.vector.tensor_copy, 3 * CHUNK, T)
         requantize(2)
-        store_words(2 * CHUNK, 3 * CHUNK, nc.scalar)
+        store_words(0, 3 * CHUNK)
         requantize(3)
         store_words(3 * CHUNK, T)
         for q in range(4):
-            queue = nc.scalar if q % 2 == 0 else nc.sync
+            queue = nc.scalar if q == 0 else nc.sync
             queue.dma_start(
                 out=out_2[0, 4 * q : 4 * q + 4, :].bitcast(I32),
                 in_=o_planes[32 * q : 32 * q + 4, :].bitcast(I32),

@@ -40,8 +40,7 @@ def tile_picked_wmedian_none_lo_kernel(tc, x_words, x_scales, w1, pos1, pos2, po
             nc.sync.dma_start(out=w_raw[0][:, 2 * u : 2 * u + 2, :], in_=w_rows[:, 2 * u : 2 * u + 2, : N // 2])
         nc.sync.dma_start(out=x_codes[:].bitcast(I32), in_=x_words[0].bitcast(I32))
         for q in range(4):
-            queue = nc.scalar if q < 2 else nc.sync
-            queue.dma_start(
+            nc.scalar.dma_start(
                 out=x_planes[32 * q : 32 * q + 4, :].bitcast(I32),
                 in_=x_scales[0, 4 * q : 4 * q + 4, :].bitcast(I32),
             )
@@ -51,9 +50,10 @@ def tile_picked_wmedian_none_lo_kernel(tc, x_words, x_scales, w1, pos1, pos2, po
         nc.sync.dma_start(lists[2][:], pos3)
 
         y = keep.tile([P, PACK * T + SPARE], F32)
-        zeros = keep.tile([P, SPARE], F32)
+        zeros = keep.tile([P, 8], F32)
         nc.vector.memset(zeros[:], 0.0)
-        nc.scalar.copy(out=y[:, PACK * T :], in_=zeros[:])
+        nc.vector.memset(y[:, PACK * T + 8 :], 0.0)
+        nc.scalar.copy(out=y[:, PACK * T : PACK * T + 8], in_=zeros[:])
 
         dealt_a = keep.tile([P, 2, M_HALF, PACK], BF16, align_bytes=64)
         dealt_b = keep.tile([P, 2, M_HALF, PACK], BF16, align_bytes=64, tag="shared")
@@ -195,10 +195,11 @@ def tile_picked_wmedian_none_lo_kernel(tc, x_words, x_scales, w1, pos1, pos2, po
         quantize_cd(1)
         project(2, 0, T, nc.scalar.copy)
         project(3, 0, T, nc.scalar.copy)
+        gather(1, 0, 1)
         finish(0)
         swap(0)
-        for args in gathers(1):
-            gather(*args)
+        gather(1, 1, 1)
+        gather(1, 2, 1)
         order_pair(1)
         ahead = gathers(2)
         cap(1)
@@ -229,11 +230,11 @@ def tile_picked_wmedian_none_lo_kernel(tc, x_words, x_scales, w1, pos1, pos2, po
         requantize(0)
         finish(last)
         requantize(1)
+        store_words(0, 2 * CHUNK)
         round_back(nc.vector.tensor_copy, 3 * CHUNK, T)
         requantize(2)
-        store_words(0, 3 * CHUNK)
         requantize(3)
-        store_words(3 * CHUNK, T)
+        store_words(2 * CHUNK, T)
         for q in range(4):
             queue = nc.scalar if q == 0 else nc.sync
             queue.dma_start(

@@ -21,7 +21,6 @@ PACK = 4
 SPARE = 176
 M_HALF = 64
 CHUNK = 128
-STEPS = [(0, T), (T, 2 * T), (2 * T, 3 * T + 2 * CHUNK), (3 * T + 2 * CHUNK, 3 * T + 3 * CHUNK), (3 * T + 3 * CHUNK, 4 * T)]
 
 
 def tile_picked_wmedian_none_lo_kernel(tc, x_words, x_scales, w1, pos1, pos2, pos3, out_0, out_1, out_2):
@@ -118,56 +117,55 @@ def tile_picked_wmedian_none_lo_kernel(tc, x_words, x_scales, w1, pos1, pos2, po
         out_words = out_1[0].rearrange("p v t -> p (v t)").bitcast(I32)
 
         work = {}
-
-        def scratch(i, kind):
-            if (i, kind) not in work:
-                e0, e1 = STEPS[i]
-                if i == 0 and kind in ("n2", "hi", "lo"):
-                    late = keep.tile([P, 3, T], F32, name="late", align_bytes=64, tag="shared")
-                    for row, name in enumerate(("n2", "hi", "lo")):
-                        work[(0, name)] = late[:, row, :]
+        for step in range(2):
+            for kind in ("n0", "n1", "n2", "hi", "lo", "mid"):
+                if (step, kind) == (0, "n1"):
+                    whole = keep.tile([P, 2 * T], F32, name="late", align_bytes=64, tag="shared")
                 else:
-                    whole = keep.tile([P, e1 - e0], F32, name=f"{kind}{i}")
-                    work[(i, kind)] = whole[:]
-            return work[(i, kind)]
+                    whole = keep.tile([P, 2 * T], F32, name=f"{kind}{step}")
+                work[(step, kind)] = whole
 
-        def gather(i, d, t):
-            e0, e1 = STEPS[i]
-            v0, v1 = max(e0 - t * T, 0), min(e1 - t * T, T)
+        def gather(d, t, v0=0, v1=T):
             window = T + SPARE if v1 - v0 == T else T
+            e0 = (t % 2) * T
             nc.vector.tensor_copy(
-                scratch(i, f"n{d}")[:, t * T + v0 - e0 : t * T + v1 - e0],
+                work[(t // 2, f"n{d}")][:, e0 + v0 : e0 + v1],
                 y[:, base(t) : base(t) + window].indirect(lists[d][:, v0 // 16 : v1 // 16]),
             )
 
-        def gathers(i):
-            e0, e1 = STEPS[i]
-            return [(i, d, t) for t in range(e0 // T, (e1 - 1) // T + 1) for d in range(3)]
+        def combine(step, dst, a, b, op, e0, e1):
+            nc.vector.tensor_tensor(work[(step, dst)][:, e0:e1], work[(step, a)][:, e0:e1], work[(step, b)][:, e0:e1], op)
 
-        def upper(i):
-            nc.vector.tensor_tensor(scratch(i, "hi"), scratch(i, "n0"), scratch(i, "n1"), MAX)
+        def upper(step, e0=0, e1=2 * T):
+            combine(step, "hi", "n0", "n1", MAX, e0, e1)
 
-        def lower(i):
-            nc.vector.tensor_tensor(scratch(i, "lo"), scratch(i, "n0"), scratch(i, "n1"), MIN)
+        def lower(step, e0=0, e1=2 * T):
+            combine(step, "lo", "n0", "n1", MIN, e0, e1)
 
-        def order_pair(i):
-            upper(i)
-            lower(i)
+        def cap(step, e0=0, e1=2 * T):
+            combine(step, "mid", "hi", "n2", MIN, e0, e1)
 
-        def cap(i):
-            nc.vector.tensor_tensor(scratch(i, "mid"), scratch(i, "hi"), scratch(i, "n2"), MIN)
+        def finish_front():
+            nc.vector.tensor_tensor(
+                front[:, 0:3:2, :],
+                work[(0, "lo")][:].rearrange("p (t v) -> p t v", t=2),
+                work[(0, "mid")][:].rearrange("p (t v) -> p t v", t=2),
+                MAX,
+            )
 
-        def finish(i):
-            e0, e1 = STEPS[i]
-            dst = front[:, 2 * i, :] if i < 2 else back[:, e0 - 2 * T : e1 - 2 * T]
-            nc.vector.tensor_tensor(dst, scratch(i, "lo"), scratch(i, "mid"), MAX)
-            if i >= 2:
-                nc.sync.dma_start(out=out_flat[:, e0:e1], in_=dst)
+        def finish_back(e0, e1):
+            nc.vector.tensor_tensor(back[:, e0:e1], work[(1, "lo")][:, e0:e1], work[(1, "mid")][:, e0:e1], MAX)
+
+        def store_back(e0, e1):
+            nc.sync.dma_start(out=out_flat[:, 2 * T + e0 : 2 * T + e1], in_=back[:, e0:e1])
 
         def swap(h):
             rows = slice(h * M_HALF, (h + 1) * M_HALF)
             other = slice((1 - h) * M_HALF, (2 - h) * M_HALF)
             nc.sync.dma_start(out=front[rows, 1, :], in_=front[other, 2 * h, :])
+
+        def hand_on_front(h):
+            rows = slice(h * M_HALF, (h + 1) * M_HALF)
             nc.sync.dma_start(out=out_flat[rows, : 2 * T], in_=front[rows, h : h + 2, :].rearrange("p t v -> p (t v)"))
             nc.scalar.copy(out=rounded[rows, :, 0:2], in_=front[rows, h : h + 2, :].rearrange("p e v -> p v e"))
 
@@ -185,50 +183,46 @@ def tile_picked_wmedian_none_lo_kernel(tc, x_words, x_scales, w1, pos1, pos2, po
         def store_words(v0, v1):
             nc.sync.dma_start(out=out_words[:, v0:v1], in_=o_codes[:, v0:v1].bitcast(I32))
 
-        gather(0, 0, 0)
-        gather(0, 1, 0)
+        gather(0, 0)
         quantize_w(dealt_b[:], P, 2 * P)
         project(1, 0, T, nc.scalar.copy)
-        gather(0, 2, 0)
-        order_pair(0)
-        cap(0)
+        gather(1, 0)
+        gather(2, 0)
         quantize_cd(1)
         project(2, 0, T, nc.scalar.copy)
         project(3, 0, T, nc.scalar.copy)
-        gather(1, 0, 1)
-        finish(0)
-        swap(0)
-        gather(1, 1, 1)
-        gather(1, 2, 1)
-        order_pair(1)
-        ahead = gathers(2)
-        cap(1)
-        gather(*ahead[0])
-        finish(1)
-        swap(1)
-        for args in ahead[1:]:
-            gather(*args)
-        order_pair(2)
-        gather(3, 0, 3)
-        cap(2)
-        gather(3, 1, 3)
-        finish(2)
+        for d in range(3):
+            gather(d, 1)
+        upper(0)
+        lower(0)
+        cap(0)
+        gather(0, 2)
+        finish_front()
+        for h in range(2):
+            swap(h)
+        for h in range(2):
+            hand_on_front(h)
+        gather(1, 2)
+        gather(0, 3)
+        gather(1, 3)
+        gather(2, 2)
+        cut = T + 2 * CHUNK
+        upper(1, 0, cut)
+        gather(2, 3, 0, 2 * CHUNK)
+        lower(1, 0, cut)
+        cap(1, 0, cut)
+        upper(1, cut, 2 * T)
+        finish_back(0, cut)
+        store_back(0, cut)
         round_back(nc.scalar.copy, 0, 2 * CHUNK)
-        upper(3)
-        gather(3, 2, 3)
-        gather(4, 0, 3)
-        gather(4, 1, 3)
-        lower(3)
-        cap(3)
-        upper(4)
-        gather(4, 2, 3)
-        finish(3)
-        round_back(nc.scalar.copy, 2 * CHUNK, 3 * CHUNK)
-        lower(4)
-        last = 4
-        cap(last)
+        gather(2, 3, 2 * CHUNK, T)
+        lower(1, cut, 2 * T)
+        cap(1, cut, 2 * T)
         requantize(0)
-        finish(last)
+        finish_back(cut, cut + CHUNK)
+        round_back(nc.scalar.copy, 2 * CHUNK, 3 * CHUNK)
+        finish_back(cut + CHUNK, 2 * T)
+        store_back(cut, 2 * T)
         requantize(1)
         store_words(0, 2 * CHUNK)
         round_back(nc.vector.tensor_copy, 3 * CHUNK, T)

@@ -37,14 +37,14 @@ def tile_picked_wmedian_none_lo_kernel(tc, x_words, x_scales, w1, pos1, pos2, po
 
         for u in range(2):
             nc.sync.dma_start(out=w_raw[0][:, 2 * u : 2 * u + 2, :], in_=w_rows[:, 2 * u : 2 * u + 2, : N // 2])
-        nc.sync.dma_start(out=x_codes[:].bitcast(I32), in_=x_words[0].bitcast(I32))
         for q in range(4):
-            nc.scalar.dma_start(
+            nc.sync.dma_start(
                 out=x_planes[32 * q : 32 * q + 4, :].bitcast(I32),
                 in_=x_scales[0, 4 * q : 4 * q + 4, :].bitcast(I32),
             )
-        nc.sync.dma_start(lists[0][:], pos1)
+        nc.sync.dma_start(out=x_codes[:].bitcast(I32), in_=x_words[0].bitcast(I32))
         nc.sync.dma_start(out=w_raw[1][:], in_=w_rows[:, :, N // 2 :])
+        nc.sync.dma_start(lists[0][:], pos1)
         nc.sync.dma_start(lists[1][:], pos2)
         nc.sync.dma_start(lists[2][:], pos3)
 
@@ -55,7 +55,7 @@ def tile_picked_wmedian_none_lo_kernel(tc, x_words, x_scales, w1, pos1, pos2, po
         nc.scalar.copy(out=y[:, PACK * T : PACK * T + 8], in_=zeros[:])
 
         dealt_a = keep.tile([P, 2, M_HALF, PACK], BF16, align_bytes=64)
-        dealt_b = keep.tile([P, 2, M_HALF, PACK], BF16, align_bytes=64, tag="shared")
+        dealt_b = keep.tile([P, 2, M_HALF, PACK], BF16, align_bytes=64)
         dealt_cd = [keep.tile([P, 2, M_HALF, PACK], BF16, align_bytes=64, name=f"dealt_cd{h}") for h in range(2)]
         w_codes = keep.tile([P, N], U32, align_bytes=64)
         w_planes = keep.tile([P, N], U8, align_bytes=64)
@@ -119,10 +119,7 @@ def tile_picked_wmedian_none_lo_kernel(tc, x_words, x_scales, w1, pos1, pos2, po
         work = {}
         for step in range(2):
             for kind in ("n0", "n1", "n2", "hi", "lo", "mid"):
-                if (step, kind) == (0, "n1"):
-                    whole = keep.tile([P, 2 * T], F32, name="late", align_bytes=64, tag="shared")
-                else:
-                    whole = keep.tile([P, 2 * T], F32, name=f"{kind}{step}")
+                whole = keep.tile([P, 2 * T], F32, name=f"{kind}{step}")
                 work[(step, kind)] = whole
 
         def gather(d, t, v0=0, v1=T):
@@ -187,10 +184,10 @@ def tile_picked_wmedian_none_lo_kernel(tc, x_words, x_scales, w1, pos1, pos2, po
         quantize_w(dealt_b[:], P, 2 * P)
         project(1, 0, T, nc.scalar.copy)
         gather(1, 0)
-        gather(2, 0)
         quantize_cd(1)
         project(2, 0, T, nc.scalar.copy)
         project(3, 0, T, nc.scalar.copy)
+        gather(2, 0)
         for d in range(3):
             gather(d, 1)
         upper(0)
@@ -207,21 +204,26 @@ def tile_picked_wmedian_none_lo_kernel(tc, x_words, x_scales, w1, pos1, pos2, po
         gather(1, 3)
         gather(2, 2)
         cut = T + 2 * CHUNK
-        upper(1, 0, cut)
+        upper(1)
         gather(2, 3, 0, 2 * CHUNK)
-        lower(1, 0, cut)
+        lower(1, 0, cut + CHUNK)
         cap(1, 0, cut)
-        upper(1, cut, 2 * T)
+        gather(2, 3, 2 * CHUNK, 3 * CHUNK)
         finish_back(0, cut)
         store_back(0, cut)
-        round_back(nc.scalar.copy, 0, 2 * CHUNK)
-        gather(2, 3, 2 * CHUNK, T)
-        lower(1, cut, 2 * T)
-        cap(1, cut, 2 * T)
-        requantize(0)
+        round_back(nc.scalar.copy, 0, CHUNK)
+        round_back(nc.scalar.copy, CHUNK, 2 * CHUNK)
+        tail = slice(cut + CHUNK, 2 * T)
+        tail_n2 = work[(1, "hi")][:, :CHUNK]
+        tail_lo = work[(1, "hi")][:, CHUNK : 2 * CHUNK]
+        nc.vector.tensor_copy(tail_n2, y[:, base(3) : base(3) + T].indirect(lists[2][:, 3 * CHUNK // 16 :]))
+        cap(1, cut, cut + CHUNK)
+        nc.vector.tensor_tensor(tail_lo, work[(1, "n0")][:, tail], work[(1, "n1")][:, tail], MIN)
+        nc.vector.tensor_tensor(work[(1, "mid")][:, tail], work[(1, "hi")][:, tail], tail_n2, MIN)
         finish_back(cut, cut + CHUNK)
         round_back(nc.scalar.copy, 2 * CHUNK, 3 * CHUNK)
-        finish_back(cut + CHUNK, 2 * T)
+        requantize(0)
+        nc.vector.tensor_tensor(back[:, tail], tail_lo, work[(1, "mid")][:, tail], MAX)
         store_back(cut, 2 * T)
         requantize(1)
         store_words(0, 2 * CHUNK)

@@ -18,9 +18,13 @@ MAX = mybir.AluOpType.max
 
 P = 128
 PACK = 4
+HALF = P // 2
+QUADRANT = 32
+LIST_ROWS = 16
 SPARE = 176
-M_HALF = 64
+EARLY = 8
 CHUNK = 128
+CUT = T + 2 * CHUNK
 
 
 def tile_picked_wmedian_none_lo_kernel(tc, x_words, x_scales, w1, pos1, pos2, pos3, out_0, out_1, out_2):
@@ -31,7 +35,7 @@ def tile_picked_wmedian_none_lo_kernel(tc, x_words, x_scales, w1, pos1, pos2, po
 
         w_rows = w1.rearrange("(p j) c -> p j c", j=PACK)
         w_raw = [keep.tile([P, PACK, N // 2], F32, name=f"w_raw{h}") for h in range(2)]
-        lists = [keep.tile([P, T // 16], U16, name=f"offsets{d}") for d in range(3)]
+        lists = [keep.tile([P, T // LIST_ROWS], U16, name=f"offsets{d}") for d in range(3)]
         x_codes = keep.tile([P, 2 * T], U8, align_bytes=64)
         x_planes = keep.tile([P, T], U8, align_bytes=64)
 
@@ -39,7 +43,7 @@ def tile_picked_wmedian_none_lo_kernel(tc, x_words, x_scales, w1, pos1, pos2, po
             nc.sync.dma_start(out=w_raw[0][:, 2 * u : 2 * u + 2, :], in_=w_rows[:, 2 * u : 2 * u + 2, : N // 2])
         for q in range(4):
             nc.sync.dma_start(
-                out=x_planes[32 * q : 32 * q + 4, :].bitcast(I32),
+                out=x_planes[QUADRANT * q : QUADRANT * q + 4, :].bitcast(I32),
                 in_=x_scales[0, 4 * q : 4 * q + 4, :].bitcast(I32),
             )
         nc.sync.dma_start(out=x_codes[:].bitcast(I32), in_=x_words[0].bitcast(I32))
@@ -49,14 +53,14 @@ def tile_picked_wmedian_none_lo_kernel(tc, x_words, x_scales, w1, pos1, pos2, po
         nc.sync.dma_start(lists[2][:], pos3)
 
         y = keep.tile([P, PACK * T + SPARE], F32)
-        zeros = keep.tile([P, 8], F32)
+        zeros = keep.tile([P, EARLY], F32)
         nc.vector.memset(zeros[:], 0.0)
-        nc.vector.memset(y[:, PACK * T + 8 :], 0.0)
-        nc.scalar.copy(out=y[:, PACK * T : PACK * T + 8], in_=zeros[:])
+        nc.vector.memset(y[:, PACK * T + EARLY :], 0.0)
+        nc.scalar.copy(out=y[:, PACK * T : PACK * T + EARLY], in_=zeros[:])
 
-        dealt_a = keep.tile([P, 2, M_HALF, PACK], BF16, align_bytes=64)
-        dealt_b = keep.tile([P, 2, M_HALF, PACK], BF16, align_bytes=64)
-        dealt_cd = [keep.tile([P, 2, M_HALF, PACK], BF16, align_bytes=64, name=f"dealt_cd{h}") for h in range(2)]
+        dealt_a = keep.tile([P, 2, HALF, PACK], BF16, align_bytes=64)
+        dealt_b = keep.tile([P, 2, HALF, PACK], BF16, align_bytes=64)
+        dealt_cd = [keep.tile([P, 2, HALF, PACK], BF16, align_bytes=64, name=f"dealt_cd{h}") for h in range(2)]
         w_codes = keep.tile([P, N], U32, align_bytes=64)
         w_planes = keep.tile([P, N], U8, align_bytes=64)
 
@@ -75,8 +79,8 @@ def tile_picked_wmedian_none_lo_kernel(tc, x_words, x_scales, w1, pos1, pos2, po
 
         def quantize_cd(h):
             for t in range(2):
-                c0 = (2 + t) * P + h * M_HALF
-                quantize_w(dealt_cd[h][:, t : t + 1], c0, c0 + M_HALF)
+                c0 = (2 + t) * P + h * HALF
+                quantize_w(dealt_cd[h][:, t : t + 1], c0, c0 + HALF)
 
         def base(t):
             return (PACK - 1 - t) * T
@@ -97,14 +101,17 @@ def tile_picked_wmedian_none_lo_kernel(tc, x_words, x_scales, w1, pos1, pos2, po
         deal(nc.vector.tensor_copy, dealt_a[:], 0, 0, 0, 2)
         deal(nc.vector.tensor_copy, dealt_cd[0][:], 0, 2, 0, 2)
         for t in range(2):
-            deal(nc.vector.tensor_copy, dealt_a[:, t : t + 1], 0, t, 2, 4, 1)
+            deal(nc.vector.tensor_copy, dealt_a[:, t : t + 1], 0, t, 2, PACK, 1)
         for t in range(2):
-            quantize_w(dealt_a[:, t : t + 1], t * M_HALF, (t + 1) * M_HALF)
-        deal(nc.scalar.copy, dealt_cd[0][:], 0, 2, 2, 4)
+            quantize_w(dealt_a[:, t : t + 1], t * HALF, (t + 1) * HALF)
+        deal(nc.scalar.copy, dealt_cd[0][:], 0, 2, 2, PACK)
         quantize_cd(0)
         for c in range(T // CHUNK):
             project(0, c * CHUNK, (c + 1) * CHUNK, nc.vector.tensor_copy)
-        deal(nc.scalar.copy, dealt_b[:], 1, 0)
+        nc.scalar.copy(
+            out=dealt_b[:].rearrange("p t m j -> p m j t"),
+            in_=w_raw[1][:].rearrange("p j (m t) -> p m j t", t=PACK)[:, :, :, 0:2],
+        )
         deal(nc.scalar.copy, dealt_cd[1][:], 1, 2)
 
         front = keep.tile([P, 3, T], F32)
@@ -122,24 +129,24 @@ def tile_picked_wmedian_none_lo_kernel(tc, x_words, x_scales, w1, pos1, pos2, po
                 whole = keep.tile([P, 2 * T], F32, name=f"{kind}{step}")
                 work[(step, kind)] = whole
 
-        def gather(d, t, v0=0, v1=T):
+        def fetch(dst, d, t, v0, v1):
             window = T + SPARE if v1 - v0 == T else T
+            nc.vector.tensor_copy(dst, y[:, base(t) : base(t) + window].indirect(lists[d][:, v0 // LIST_ROWS : v1 // LIST_ROWS]))
+
+        def gather(d, t, v0=0, v1=T):
             e0 = (t % 2) * T
-            nc.vector.tensor_copy(
-                work[(t // 2, f"n{d}")][:, e0 + v0 : e0 + v1],
-                y[:, base(t) : base(t) + window].indirect(lists[d][:, v0 // 16 : v1 // 16]),
-            )
+            fetch(work[(t // 2, f"n{d}")][:, e0 + v0 : e0 + v1], d, t, v0, v1)
 
         def combine(step, dst, a, b, op, e0, e1):
             nc.vector.tensor_tensor(work[(step, dst)][:, e0:e1], work[(step, a)][:, e0:e1], work[(step, b)][:, e0:e1], op)
 
-        def upper(step, e0=0, e1=2 * T):
-            combine(step, "hi", "n0", "n1", MAX, e0, e1)
+        def upper(step):
+            combine(step, "hi", "n0", "n1", MAX, 0, 2 * T)
 
-        def lower(step, e0=0, e1=2 * T):
+        def lower(step, e0, e1):
             combine(step, "lo", "n0", "n1", MIN, e0, e1)
 
-        def cap(step, e0=0, e1=2 * T):
+        def cap(step, e0, e1):
             combine(step, "mid", "hi", "n2", MIN, e0, e1)
 
         def finish_front():
@@ -157,17 +164,18 @@ def tile_picked_wmedian_none_lo_kernel(tc, x_words, x_scales, w1, pos1, pos2, po
             nc.sync.dma_start(out=out_flat[:, 2 * T + e0 : 2 * T + e1], in_=back[:, e0:e1])
 
         def swap(h):
-            rows = slice(h * M_HALF, (h + 1) * M_HALF)
-            other = slice((1 - h) * M_HALF, (2 - h) * M_HALF)
+            rows = slice(h * HALF, (h + 1) * HALF)
+            other = slice((1 - h) * HALF, (2 - h) * HALF)
             nc.sync.dma_start(out=front[rows, 1, :], in_=front[other, 2 * h, :])
 
         def hand_on_front(h):
-            rows = slice(h * M_HALF, (h + 1) * M_HALF)
+            rows = slice(h * HALF, (h + 1) * HALF)
             nc.sync.dma_start(out=out_flat[rows, : 2 * T], in_=front[rows, h : h + 2, :].rearrange("p t v -> p (t v)"))
             nc.scalar.copy(out=rounded[rows, :, 0:2], in_=front[rows, h : h + 2, :].rearrange("p e v -> p v e"))
 
-        def round_back(copy, v0, v1):
-            copy(out=rounded[:, v0:v1, 2:4], in_=back_rows[:, :, v0:v1].rearrange("p e v -> p v e"))
+        def round_back(copy, c):
+            cols = slice(c * CHUNK, (c + 1) * CHUNK)
+            copy(out=rounded[:, cols, 2:PACK], in_=back_rows[:, :, cols].rearrange("p e v -> p v e"))
 
         def requantize(c):
             cols = slice(c * CHUNK, (c + 1) * CHUNK)
@@ -191,49 +199,51 @@ def tile_picked_wmedian_none_lo_kernel(tc, x_words, x_scales, w1, pos1, pos2, po
         for d in range(3):
             gather(d, 1)
         upper(0)
-        lower(0)
-        cap(0)
+        lower(0, 0, 2 * T)
+        cap(0, 0, 2 * T)
         gather(0, 2)
         finish_front()
         for h in range(2):
             swap(h)
         for h in range(2):
             hand_on_front(h)
+
         gather(1, 2)
         gather(0, 3)
         gather(1, 3)
         gather(2, 2)
-        cut = T + 2 * CHUNK
         upper(1)
         gather(2, 3, 0, 2 * CHUNK)
-        lower(1, 0, cut + CHUNK)
-        cap(1, 0, cut)
+        lower(1, 0, CUT + CHUNK)
+        cap(1, 0, CUT)
         gather(2, 3, 2 * CHUNK, 3 * CHUNK)
-        finish_back(0, cut)
-        store_back(0, cut)
-        round_back(nc.scalar.copy, 0, CHUNK)
-        round_back(nc.scalar.copy, CHUNK, 2 * CHUNK)
-        tail = slice(cut + CHUNK, 2 * T)
-        tail_n2 = work[(1, "hi")][:, :CHUNK]
-        tail_lo = work[(1, "hi")][:, CHUNK : 2 * CHUNK]
-        nc.vector.tensor_copy(tail_n2, y[:, base(3) : base(3) + T].indirect(lists[2][:, 3 * CHUNK // 16 :]))
-        cap(1, cut, cut + CHUNK)
-        nc.vector.tensor_tensor(tail_lo, work[(1, "n0")][:, tail], work[(1, "n1")][:, tail], MIN)
-        nc.vector.tensor_tensor(work[(1, "mid")][:, tail], work[(1, "hi")][:, tail], tail_n2, MIN)
-        finish_back(cut, cut + CHUNK)
-        round_back(nc.scalar.copy, 2 * CHUNK, 3 * CHUNK)
+        finish_back(0, CUT)
+        store_back(0, CUT)
+        round_back(nc.scalar.copy, 0)
+        round_back(nc.scalar.copy, 1)
+
+        last = slice(CUT + CHUNK, 2 * T)
+        last_n2 = work[(1, "hi")][:, :CHUNK]
+        last_lo = work[(1, "hi")][:, CHUNK : 2 * CHUNK]
+        fetch(last_n2, 2, 3, 3 * CHUNK, T)
+        cap(1, CUT, CUT + CHUNK)
+        nc.vector.tensor_tensor(last_lo, work[(1, "n0")][:, last], work[(1, "n1")][:, last], MIN)
+        nc.vector.tensor_tensor(work[(1, "mid")][:, last], work[(1, "hi")][:, last], last_n2, MIN)
+        finish_back(CUT, CUT + CHUNK)
+        round_back(nc.scalar.copy, 2)
         requantize(0)
-        nc.vector.tensor_tensor(back[:, tail], tail_lo, work[(1, "mid")][:, tail], MAX)
-        store_back(cut, 2 * T)
+        nc.vector.tensor_tensor(back[:, last], last_lo, work[(1, "mid")][:, last], MAX)
+        store_back(CUT, 2 * T)
         requantize(1)
         store_words(0, 2 * CHUNK)
-        round_back(nc.vector.tensor_copy, 3 * CHUNK, T)
+        round_back(nc.vector.tensor_copy, 3)
         requantize(2)
         requantize(3)
         store_words(2 * CHUNK, T)
+
         for q in range(4):
             queue = nc.scalar if q == 0 else nc.sync
             queue.dma_start(
                 out=out_2[0, 4 * q : 4 * q + 4, :].bitcast(I32),
-                in_=o_planes[32 * q : 32 * q + 4, :].bitcast(I32),
+                in_=o_planes[QUADRANT * q : QUADRANT * q + 4, :].bitcast(I32),
             )

@@ -121,6 +121,7 @@ def tile_picked_wmedian_none_lo_kernel(tc, x_words, x_scales, w1, pos1, pos2, po
         o_codes = keep.tile([P, T], U32, align_bytes=64)
         o_planes = keep.tile([P, T], U8, align_bytes=64)
         out_flat = out_0.rearrange("(p t) v -> p (t v)", t=PACK)
+        out_rows = out_0.rearrange("(p t) v -> p t v", t=PACK)
         out_words = out_1[0].rearrange("p v t -> p (v t)").bitcast(I32)
 
         work = {}
@@ -156,12 +157,6 @@ def tile_picked_wmedian_none_lo_kernel(tc, x_words, x_scales, w1, pos1, pos2, po
                 work[(0, "mid")][:].rearrange("p (t v) -> p t v", t=2),
                 MAX,
             )
-
-        def finish_back(e0, e1):
-            nc.vector.tensor_tensor(back[:, e0:e1], work[(1, "lo")][:, e0:e1], work[(1, "mid")][:, e0:e1], MAX)
-
-        def store_back(e0, e1):
-            nc.sync.dma_start(out=out_flat[:, 2 * T + e0 : 2 * T + e1], in_=back[:, e0:e1])
 
         def swap(h):
             rows = slice(h * HALF, (h + 1) * HALF)
@@ -208,32 +203,38 @@ def tile_picked_wmedian_none_lo_kernel(tc, x_words, x_scales, w1, pos1, pos2, po
         for h in range(2):
             hand_on_front(h)
 
+        def both(kind, v0, v1):
+            return work[(1, kind)][:].rearrange("p (t v) -> p t v", t=2)[:, :, v0:v1]
+
+        def late(dst, a, b, op, v0, v1):
+            nc.vector.tensor_tensor(both(dst, v0, v1), both(a, v0, v1), both(b, v0, v1), op)
+
+        def finish_late(v0, v1):
+            nc.vector.tensor_tensor(back_rows[:, :, v0:v1], both("lo", v0, v1), both("mid", v0, v1), MAX)
+
+        def store_late(v0, v1):
+            nc.sync.dma_start(out=out_rows[:, 2:PACK, v0:v1], in_=back_rows[:, :, v0:v1])
+
         gather(1, 2)
         gather(0, 3)
         gather(1, 3)
         gather(2, 2)
         upper(1)
-        gather(2, 3, 0, 2 * CHUNK)
-        lower(1, 0, CUT + CHUNK)
-        cap(1, 0, CUT)
-        gather(2, 3, 2 * CHUNK, 3 * CHUNK)
-        finish_back(0, CUT)
-        store_back(0, CUT)
+        gather(2, 3)
+        late("lo", "n0", "n1", MIN, 0, 2 * CHUNK)
+        late("mid", "hi", "n2", MIN, 0, 2 * CHUNK)
+        late("lo", "n0", "n1", MIN, 2 * CHUNK, T)
+        finish_late(0, 2 * CHUNK)
+        store_late(0, 2 * CHUNK)
         round_back(nc.scalar.copy, 0)
         round_back(nc.scalar.copy, 1)
-
-        last = slice(CUT + CHUNK, 2 * T)
-        last_n2 = work[(1, "hi")][:, :CHUNK]
-        last_lo = work[(1, "hi")][:, CHUNK : 2 * CHUNK]
-        fetch(last_n2, 2, 3, 3 * CHUNK, T)
-        cap(1, CUT, CUT + CHUNK)
-        nc.vector.tensor_tensor(last_lo, work[(1, "n0")][:, last], work[(1, "n1")][:, last], MIN)
-        nc.vector.tensor_tensor(work[(1, "mid")][:, last], work[(1, "hi")][:, last], last_n2, MIN)
-        finish_back(CUT, CUT + CHUNK)
+        late("mid", "hi", "n2", MIN, 2 * CHUNK, 3 * CHUNK)
+        late("mid", "hi", "n2", MIN, 3 * CHUNK, T)
+        finish_late(2 * CHUNK, 3 * CHUNK)
         round_back(nc.scalar.copy, 2)
+        finish_late(3 * CHUNK, T)
+        store_late(2 * CHUNK, T)
         requantize(0)
-        nc.vector.tensor_tensor(back[:, last], last_lo, work[(1, "mid")][:, last], MAX)
-        store_back(CUT, 2 * T)
         requantize(1)
         store_words(0, 2 * CHUNK)
         round_back(nc.vector.tensor_copy, 3)

@@ -53,10 +53,7 @@ def tile_picked_wmedian_none_lo_kernel(tc, x_words, x_scales, w1, pos1, pos2, po
         nc.sync.dma_start(lists[2][:], pos3)
 
         y = keep.tile([P, PACK * T + SPARE], F32)
-        zeros = keep.tile([P, EARLY], F32)
-        nc.vector.memset(zeros[:], 0.0)
-        nc.vector.memset(y[:, PACK * T + EARLY :], 0.0)
-        nc.scalar.copy(out=y[:, PACK * T : PACK * T + EARLY], in_=zeros[:])
+        nc.vector.memset(y[:, PACK * T :], 0.0)
 
         dealt_a = keep.tile([P, 2, HALF, PACK], BF16, align_bytes=64)
         dealt_b = keep.tile([P, 2, HALF, PACK], BF16, align_bytes=64)

@@ -17,6 +17,7 @@ MIN = mybir.AluOpType.min
 MAX = mybir.AluOpType.max
 
 P = 128
+ALIGN = 256
 PACK = 4
 HALF = P // 2
 QUADRANT = 32
@@ -34,10 +35,10 @@ def tile_picked_wmedian_none_lo_kernel(tc, x_words, x_scales, w1, pos1, pos2, po
         psum = ctx.enter_context(tc.psum_pool(name="psum", bufs=1))
 
         w_rows = w1.rearrange("(p j) c -> p j c", j=PACK)
-        w_raw = [keep.tile([P, PACK, N // 2], F32, name=f"w_raw{h}") for h in range(2)]
+        w_raw = [keep.tile([P, PACK, N // 2], F32, align_bytes=ALIGN, name=f"w_raw{h}") for h in range(2)]
         lists = [keep.tile([P, T // LIST_ROWS], U16, name=f"offsets{d}") for d in range(3)]
-        x_codes = keep.tile([P, 2 * T], U8, align_bytes=64)
-        x_planes = keep.tile([P, T], U8, align_bytes=64)
+        x_codes = keep.tile([P, 2 * T], U8, align_bytes=ALIGN)
+        x_planes = keep.tile([P, T], U8, align_bytes=ALIGN)
 
         for u in range(2):
             nc.sync.dma_start(out=w_raw[0][:, 2 * u : 2 * u + 2, :], in_=w_rows[:, 2 * u : 2 * u + 2, : N // 2])
@@ -52,14 +53,14 @@ def tile_picked_wmedian_none_lo_kernel(tc, x_words, x_scales, w1, pos1, pos2, po
         nc.sync.dma_start(lists[1][:], pos2)
         nc.sync.dma_start(lists[2][:], pos3)
 
-        y = keep.tile([P, PACK * T + SPARE], F32)
+        y = keep.tile([P, PACK * T + SPARE], F32, align_bytes=ALIGN)
         nc.vector.memset(y[:, PACK * T :], 0.0)
 
-        dealt_a = keep.tile([P, 2, HALF, PACK], BF16, align_bytes=64)
-        dealt_b = keep.tile([P, 2, HALF, PACK], BF16, align_bytes=64)
-        dealt_cd = [keep.tile([P, 2, HALF, PACK], BF16, align_bytes=64, name=f"dealt_cd{h}") for h in range(2)]
-        w_codes = keep.tile([P, N], U32, align_bytes=64)
-        w_planes = keep.tile([P, N], U8, align_bytes=64)
+        dealt_a = keep.tile([P, 2, HALF, PACK], BF16, align_bytes=ALIGN)
+        dealt_b = keep.tile([P, 2, HALF, PACK], BF16, align_bytes=ALIGN)
+        dealt_cd = [keep.tile([P, 2, HALF, PACK], BF16, align_bytes=ALIGN, name=f"dealt_cd{h}") for h in range(2)]
+        w_codes = keep.tile([P, N], U32, align_bytes=ALIGN)
+        w_planes = keep.tile([P, N], U8, align_bytes=ALIGN)
 
         def deal(copy, dst, h, t0, j0=0, j1=PACK, slots=2):
             copy(
@@ -111,12 +112,12 @@ def tile_picked_wmedian_none_lo_kernel(tc, x_words, x_scales, w1, pos1, pos2, po
         )
         deal(nc.scalar.copy, dealt_cd[1][:], 1, 2)
 
-        front = keep.tile([P, 3, T], F32)
-        back = keep.tile([P, 2 * T], F32)
+        front = keep.tile([P, 3, T], F32, align_bytes=ALIGN)
+        back = keep.tile([P, 2 * T], F32, align_bytes=ALIGN)
         back_rows = back[:].rearrange("p (t v) -> p t v", t=2)
-        rounded = keep.tile([P, T, PACK], BF16, align_bytes=64)
-        o_codes = keep.tile([P, T], U32, align_bytes=64)
-        o_planes = keep.tile([P, T], U8, align_bytes=64)
+        rounded = keep.tile([P, T, PACK], BF16, align_bytes=ALIGN)
+        o_codes = keep.tile([P, T], U32, align_bytes=ALIGN)
+        o_planes = keep.tile([P, T], U8, align_bytes=ALIGN)
         out_flat = out_0.rearrange("(p t) v -> p (t v)", t=PACK)
         out_rows = out_0.rearrange("(p t) v -> p t v", t=PACK)
         out_words = out_1[0].rearrange("p v t -> p (v t)").bitcast(I32)
@@ -124,7 +125,7 @@ def tile_picked_wmedian_none_lo_kernel(tc, x_words, x_scales, w1, pos1, pos2, po
         work = {}
         for step in range(2):
             for kind in ("n0", "n1", "n2", "hi", "lo", "mid"):
-                whole = keep.tile([P, 2 * T], F32, name=f"{kind}{step}")
+                whole = keep.tile([P, 2 * T], F32, align_bytes=ALIGN, name=f"{kind}{step}")
                 work[(step, kind)] = whole
 
         def fetch(dst, d, t, v0, v1):

@@ -210,6 +210,12 @@ def tile_picked_wmedian_none_lo_kernel(tc, x_words, x_scales, w1, pos1, pos2, po
         def finish_late(v0, v1):
             nc.vector.tensor_tensor(back_rows[:, :, v0:v1], both("lo", v0, v1), both("mid", v0, v1), MAX)
 
+        def finish_flat(e0, e1):
+            nc.vector.tensor_tensor(back[:, e0:e1], work[(1, "lo")][:, e0:e1], work[(1, "mid")][:, e0:e1], MAX)
+
+        def store_flat(e0, e1):
+            nc.sync.dma_start(out=out_flat[:, 2 * T + e0 : 2 * T + e1], in_=back[:, e0:e1])
+
         def store_late(v0, v1):
             nc.sync.dma_start(out=out_rows[:, 2:PACK, v0:v1], in_=back_rows[:, :, v0:v1])
 
@@ -226,12 +232,14 @@ def tile_picked_wmedian_none_lo_kernel(tc, x_words, x_scales, w1, pos1, pos2, po
         store_late(0, 2 * CHUNK)
         round_back(nc.scalar.copy, 0)
         round_back(nc.scalar.copy, 1)
-        late("mid", "hi", "n2", MIN, 2 * CHUNK, 3 * CHUNK)
-        late("mid", "hi", "n2", MIN, 3 * CHUNK, T)
-        finish_late(2 * CHUNK, 3 * CHUNK)
+        cap(1, 2 * CHUNK, T)
+        cap(1, T + 2 * CHUNK, 2 * T)
+        finish_flat(2 * CHUNK, T)
+        store_flat(2 * CHUNK, T)
+        finish_flat(T + 2 * CHUNK, T + 3 * CHUNK)
         round_back(nc.scalar.copy, 2)
-        finish_late(3 * CHUNK, T)
-        store_late(2 * CHUNK, T)
+        finish_flat(T + 3 * CHUNK, 2 * T)
+        store_flat(T + 2 * CHUNK, 2 * T)
         requantize(0)
         requantize(1)
         store_words(0, 2 * CHUNK)

@@ -15,6 +15,7 @@ FP8X4 = mybir.dt.float8_e4m3fn_x4
 FP4X4 = mybir.dt.float4_e2m1fn_x4
 MIN = mybir.AluOpType.min
 MAX = mybir.AluOpType.max
+COPY = mybir.ActivationFunctionType.Copy
 
 P = 128
 ALIGN = 256
@@ -22,10 +23,8 @@ PACK = 4
 HALF = P // 2
 QUADRANT = 32
 LIST_ROWS = 16
-SPARE = 176
-EARLY = 8
+SPARE = 192
 CHUNK = 128
-CUT = T + 2 * CHUNK
 
 
 def tile_picked_wmedian_none_lo_kernel(tc, x_words, x_scales, w1, pos1, pos2, pos3, out_0, out_1, out_2):
@@ -53,8 +52,7 @@ def tile_picked_wmedian_none_lo_kernel(tc, x_words, x_scales, w1, pos1, pos2, po
         nc.sync.dma_start(lists[1][:], pos2)
         nc.sync.dma_start(lists[2][:], pos3)
 
-        y = keep.tile([P, PACK * T + SPARE], F32, align_bytes=ALIGN)
-        nc.vector.memset(y[:, PACK * T :], 0.0)
+        y = [keep.tile([P, T + SPARE], F32, align_bytes=ALIGN, name=f"y{t}") for t in range(PACK)]
 
         dealt_a = keep.tile([P, 2, HALF, PACK], BF16, align_bytes=ALIGN)
         dealt_b = keep.tile([P, 2, HALF, PACK], BF16, align_bytes=ALIGN)
@@ -80,10 +78,9 @@ def tile_picked_wmedian_none_lo_kernel(tc, x_words, x_scales, w1, pos1, pos2, po
                 c0 = (2 + t) * P + h * HALF
                 quantize_w(dealt_cd[h][:, t : t + 1], c0, c0 + HALF)
 
-        def base(t):
-            return (PACK - 1 - t) * T
+        banks = {}
 
-        def project(t, c0, c1, copy):
+        def project(t, c0, c1):
             bank = psum.tile([P, c1 - c0], F32, name=f"bank{t}_{c0}")
             nc.tensor.matmul_mx(
                 out=bank[:],
@@ -94,7 +91,10 @@ def tile_picked_wmedian_none_lo_kernel(tc, x_words, x_scales, w1, pos1, pos2, po
                 start=True,
                 stop=True,
             )
-            copy(out=y[:, base(t) + c0 : base(t) + c1], in_=bank[:])
+            banks[(t, c0)] = bank
+
+        def empty(copy, t, c0, c1):
+            copy(out=y[t][:, c0:c1], in_=banks[(t, c0)][:])
 
         deal(nc.vector.tensor_copy, dealt_a[:], 0, 0, 0, 2)
         deal(nc.vector.tensor_copy, dealt_cd[0][:], 0, 2, 0, 2)
@@ -105,16 +105,12 @@ def tile_picked_wmedian_none_lo_kernel(tc, x_words, x_scales, w1, pos1, pos2, po
         deal(nc.scalar.copy, dealt_cd[0][:], 0, 2, 2, PACK)
         quantize_cd(0)
         for c in range(T // CHUNK):
-            project(0, c * CHUNK, (c + 1) * CHUNK, nc.vector.tensor_copy)
-        nc.scalar.copy(
-            out=dealt_b[:].rearrange("p t m j -> p m j t"),
-            in_=w_raw[1][:].rearrange("p j (m t) -> p m j t", t=PACK)[:, :, :, 0:2],
-        )
-        deal(nc.scalar.copy, dealt_cd[1][:], 1, 2)
+            project(0, c * CHUNK, (c + 1) * CHUNK)
+            empty(nc.vector.tensor_copy, 0, c * CHUNK, (c + 1) * CHUNK)
 
-        front = keep.tile([P, 3, T], F32, align_bytes=ALIGN)
-        back = keep.tile([P, 2 * T], F32, align_bytes=ALIGN)
-        back_rows = back[:].rearrange("p (t v) -> p t v", t=2)
+        res = keep.tile([P, PACK * T], F32, align_bytes=ALIGN)
+        res_rows = res[:].rearrange("p (t v) -> p t v", t=PACK)
+        spill = keep.tile([P, T], F32, align_bytes=ALIGN)
         rounded = keep.tile([P, T, PACK], BF16, align_bytes=ALIGN)
         o_codes = keep.tile([P, T], U32, align_bytes=ALIGN)
         o_planes = keep.tile([P, T], U8, align_bytes=ALIGN)
@@ -128,78 +124,23 @@ def tile_picked_wmedian_none_lo_kernel(tc, x_words, x_scales, w1, pos1, pos2, po
                 whole = keep.tile([P, 2 * T], F32, align_bytes=ALIGN, name=f"{kind}{step}")
                 work[(step, kind)] = whole
 
-        def fetch(dst, d, t, v0, v1):
-            window = T + SPARE if v1 - v0 == T else T
-            nc.vector.tensor_copy(dst, y[:, base(t) : base(t) + window].indirect(lists[d][:, v0 // LIST_ROWS : v1 // LIST_ROWS]))
+        def part(kind, t, v0, v1):
+            return work[(t // 2, kind)][:, (t % 2) * T + v0 : (t % 2) * T + v1]
 
-        def gather(d, t, v0=0, v1=T):
-            e0 = (t % 2) * T
-            fetch(work[(t // 2, f"n{d}")][:, e0 + v0 : e0 + v1], d, t, v0, v1)
+        def looked_up(d, t, v0, v1):
+            return y[t][:].indirect(lists[d][:, v0 // LIST_ROWS : v1 // LIST_ROWS])
 
-        def combine(step, dst, a, b, op, e0, e1):
-            nc.vector.tensor_tensor(work[(step, dst)][:, e0:e1], work[(step, a)][:, e0:e1], work[(step, b)][:, e0:e1], op)
+        def gather_s(d, t, v0=0, v1=T):
+            nc.scalar.activation(part(f"n{d}", t, v0, v1), looked_up(d, t, v0, v1), COPY)
 
-        def upper(step):
-            combine(step, "hi", "n0", "n1", MAX, 0, 2 * T)
+        def gather_v(d, t, v0=0, v1=T):
+            nc.vector.tensor_copy(part(f"n{d}", t, v0, v1), looked_up(d, t, v0, v1))
 
-        def lower(step, e0, e1):
-            combine(step, "lo", "n0", "n1", MIN, e0, e1)
+        def one(dst, a, b, op, t):
+            nc.vector.tensor_tensor(part(dst, t, 0, T), part(a, t, 0, T), part(b, t, 0, T), op)
 
-        def cap(step, e0, e1):
-            combine(step, "mid", "hi", "n2", MIN, e0, e1)
-
-        def finish_front():
-            nc.vector.tensor_tensor(
-                front[:, 0:3:2, :],
-                work[(0, "lo")][:].rearrange("p (t v) -> p t v", t=2),
-                work[(0, "mid")][:].rearrange("p (t v) -> p t v", t=2),
-                MAX,
-            )
-
-        def swap(h):
-            rows = slice(h * HALF, (h + 1) * HALF)
-            other = slice((1 - h) * HALF, (2 - h) * HALF)
-            nc.sync.dma_start(out=front[rows, 1, :], in_=front[other, 2 * h, :])
-
-        def hand_on_front(h):
-            rows = slice(h * HALF, (h + 1) * HALF)
-            nc.sync.dma_start(out=out_flat[rows, : 2 * T], in_=front[rows, h : h + 2, :].rearrange("p t v -> p (t v)"))
-            nc.scalar.copy(out=rounded[rows, :, 0:2], in_=front[rows, h : h + 2, :].rearrange("p e v -> p v e"))
-
-        def round_back(copy, c):
-            cols = slice(c * CHUNK, (c + 1) * CHUNK)
-            copy(out=rounded[:, cols, 2:PACK], in_=back_rows[:, :, cols].rearrange("p e v -> p v e"))
-
-        def requantize(c):
-            cols = slice(c * CHUNK, (c + 1) * CHUNK)
-            nc.vector.quantize_mx(
-                out=o_codes[:, cols].bitcast(FP8X4),
-                scales=o_planes[:, cols],
-                in_=rounded[:, cols, :].rearrange("p v t -> p (v t)"),
-            )
-
-        def store_words(v0, v1):
-            nc.sync.dma_start(out=out_words[:, v0:v1], in_=o_codes[:, v0:v1].bitcast(I32))
-
-        gather(0, 0)
-        quantize_w(dealt_b[:], P, 2 * P)
-        project(1, 0, T, nc.scalar.copy)
-        gather(1, 0)
-        quantize_cd(1)
-        project(2, 0, T, nc.scalar.copy)
-        project(3, 0, T, nc.scalar.copy)
-        gather(2, 0)
-        for d in range(3):
-            gather(d, 1)
-        upper(0)
-        lower(0, 0, 2 * T)
-        cap(0, 0, 2 * T)
-        gather(0, 2)
-        finish_front()
-        for h in range(2):
-            swap(h)
-        for h in range(2):
-            hand_on_front(h)
+        def finish_one(t, dst):
+            nc.vector.tensor_tensor(dst, part("lo", t, 0, T), part("mid", t, 0, T), MAX)
 
         def both(kind, v0, v1):
             return work[(1, kind)][:].rearrange("p (t v) -> p t v", t=2)[:, :, v0:v1]
@@ -208,44 +149,77 @@ def tile_picked_wmedian_none_lo_kernel(tc, x_words, x_scales, w1, pos1, pos2, po
             nc.vector.tensor_tensor(both(dst, v0, v1), both(a, v0, v1), both(b, v0, v1), op)
 
         def finish_late(v0, v1):
-            nc.vector.tensor_tensor(back_rows[:, :, v0:v1], both("lo", v0, v1), both("mid", v0, v1), MAX)
-
-        def finish_flat(e0, e1):
-            nc.vector.tensor_tensor(back[:, e0:e1], work[(1, "lo")][:, e0:e1], work[(1, "mid")][:, e0:e1], MAX)
-
-        def store_flat(e0, e1):
-            nc.sync.dma_start(out=out_flat[:, 2 * T + e0 : 2 * T + e1], in_=back[:, e0:e1])
+            nc.vector.tensor_tensor(res_rows[:, 2:PACK, v0:v1], both("lo", v0, v1), both("mid", v0, v1), MAX)
 
         def store_late(v0, v1):
-            nc.sync.dma_start(out=out_rows[:, 2:PACK, v0:v1], in_=back_rows[:, :, v0:v1])
+            nc.sync.dma_start(out=out_rows[:, 2:PACK, v0:v1], in_=res_rows[:, 2:PACK, v0:v1])
 
-        gather(1, 2)
-        gather(0, 3)
-        gather(1, 3)
-        gather(2, 2)
-        upper(1)
-        gather(2, 3)
+        def round_to(copy, v0, v1):
+            copy(out=rounded[:, v0:v1, :], in_=res_rows[:, :, v0:v1].rearrange("p t v -> p v t"))
+
+        def requantize(v0, v1):
+            nc.vector.quantize_mx(
+                out=o_codes[:, v0:v1].bitcast(FP8X4),
+                scales=o_planes[:, v0:v1],
+                in_=rounded[:, v0:v1, :].rearrange("p v t -> p (v t)"),
+            )
+
+        def store_words(v0, v1):
+            nc.sync.dma_start(out=out_words[:, v0:v1], in_=o_codes[:, v0:v1].bitcast(I32))
+
+        low = slice(0, HALF)
+        high = slice(HALF, P)
+
+        gather_s(0, 0)
+        gather_s(1, 0)
+        deal(nc.vector.tensor_copy, dealt_b[:], 1, 0)
+        deal(nc.vector.tensor_copy, dealt_cd[1][:], 1, 2)
+        quantize_w(dealt_b[:], P, 2 * P)
+        quantize_cd(1)
+        for t in range(1, PACK):
+            project(t, 0, T)
+        empty(nc.vector.tensor_copy, 1, 0, T)
+        gather_v(2, 0)
+        for d in range(3):
+            gather_s(d, 1)
+        one("hi", "n0", "n1", MAX, 0)
+        one("lo", "n0", "n1", MIN, 0)
+        empty(nc.vector.tensor_copy, 2, 0, T)
+        one("mid", "hi", "n2", MIN, 0)
+        empty(nc.vector.tensor_copy, 3, 0, T)
+        finish_one(0, res[:, :T])
+        nc.sync.dma_start(out=res[low, T : 2 * T], in_=res[high, :T])
+        one("hi", "n0", "n1", MAX, 1)
+        one("lo", "n0", "n1", MIN, 1)
+        one("mid", "hi", "n2", MIN, 1)
+        pieces = ((0, 2 * CHUNK), (2 * CHUNK, T))
+        for v0, v1 in pieces:
+            for d in range(3):
+                for t in range(2, PACK):
+                    gather_s(d, t, v0, v1)
+        late("hi", "n0", "n1", MAX, 0, 2 * CHUNK)
+        finish_one(1, spill[:])
+        nc.sync.dma_start(out=res[high, :T], in_=spill[low, :])
+        nc.sync.dma_start(out=res[high, T : 2 * T], in_=spill[high, :])
+        nc.sync.dma_start(out=out_flat[:, : 2 * T], in_=res[:, : 2 * T])
         late("lo", "n0", "n1", MIN, 0, 2 * CHUNK)
         late("mid", "hi", "n2", MIN, 0, 2 * CHUNK)
-        late("lo", "n0", "n1", MIN, 2 * CHUNK, T)
         finish_late(0, 2 * CHUNK)
         store_late(0, 2 * CHUNK)
-        round_back(nc.scalar.copy, 0)
-        round_back(nc.scalar.copy, 1)
-        cap(1, 2 * CHUNK, T)
-        cap(1, T + 2 * CHUNK, 2 * T)
-        finish_flat(2 * CHUNK, T)
-        store_flat(2 * CHUNK, T)
-        finish_flat(T + 2 * CHUNK, T + 3 * CHUNK)
-        round_back(nc.scalar.copy, 2)
-        finish_flat(T + 3 * CHUNK, 2 * T)
-        store_flat(T + 2 * CHUNK, 2 * T)
-        requantize(0)
-        requantize(1)
+        late("hi", "n0", "n1", MAX, 2 * CHUNK, T)
+        round_to(nc.vector.tensor_copy, 0, 2 * CHUNK)
+        late("lo", "n0", "n1", MIN, 2 * CHUNK, T)
+        requantize(0, 2 * CHUNK)
         store_words(0, 2 * CHUNK)
-        round_back(nc.vector.tensor_copy, 3)
-        requantize(2)
-        requantize(3)
+        late("mid", "hi", "n2", MIN, 2 * CHUNK, 3 * CHUNK)
+        late("mid", "hi", "n2", MIN, 3 * CHUNK, T)
+        finish_late(2 * CHUNK, 3 * CHUNK)
+        round_to(nc.scalar.copy, 2 * CHUNK, 3 * CHUNK)
+        finish_late(3 * CHUNK, T)
+        store_late(2 * CHUNK, T)
+        round_to(nc.vector.tensor_copy, 3 * CHUNK, T)
+        requantize(2 * CHUNK, 3 * CHUNK)
+        requantize(3 * CHUNK, T)
         store_words(2 * CHUNK, T)
 
         for q in range(4):

@@ -106,7 +106,7 @@ def tile_picked_wmedian_none_lo_kernel(tc, x_words, x_scales, w1, pos1, pos2, po
         quantize_cd(0)
         for c in range(T // CHUNK):
             project(0, c * CHUNK, (c + 1) * CHUNK)
-            empty(nc.vector.tensor_copy, 0, c * CHUNK, (c + 1) * CHUNK)
+            empty(nc.scalar.copy if c % 2 else nc.vector.tensor_copy, 0, c * CHUNK, (c + 1) * CHUNK)
 
         res = keep.tile([P, PACK * T], F32, align_bytes=ALIGN)
         res_rows = res[:].rearrange("p (t v) -> p t v", t=PACK)
@@ -170,56 +170,61 @@ def tile_picked_wmedian_none_lo_kernel(tc, x_words, x_scales, w1, pos1, pos2, po
         low = slice(0, HALF)
         high = slice(HALF, P)
 
+        deal(nc.vector.tensor_copy, dealt_b[:], 1, 0)
         gather_s(0, 0)
         gather_s(1, 0)
-        deal(nc.vector.tensor_copy, dealt_b[:], 1, 0)
         deal(nc.vector.tensor_copy, dealt_cd[1][:], 1, 2)
         quantize_w(dealt_b[:], P, 2 * P)
         quantize_cd(1)
         for t in range(1, PACK):
             project(t, 0, T)
-        empty(nc.vector.tensor_copy, 1, 0, T)
+        empty(nc.scalar.copy, 1, 0, T)
         gather_v(2, 0)
-        for d in range(3):
+        for d in range(2):
             gather_s(d, 1)
+        for t in range(2, PACK):
+            empty(nc.scalar.copy, t, 0, T)
         one("hi", "n0", "n1", MAX, 0)
         one("lo", "n0", "n1", MIN, 0)
-        empty(nc.vector.tensor_copy, 2, 0, T)
         one("mid", "hi", "n2", MIN, 0)
-        empty(nc.vector.tensor_copy, 3, 0, T)
+        gather_v(2, 1)
         finish_one(0, res[:, :T])
         nc.sync.dma_start(out=res[low, T : 2 * T], in_=res[high, :T])
         one("hi", "n0", "n1", MAX, 1)
         one("lo", "n0", "n1", MIN, 1)
         one("mid", "hi", "n2", MIN, 1)
-        pieces = ((0, 2 * CHUNK), (2 * CHUNK, T))
-        for v0, v1 in pieces:
-            for d in range(3):
-                for t in range(2, PACK):
-                    gather_s(d, t, v0, v1)
-        late("hi", "n0", "n1", MAX, 0, 2 * CHUNK)
+        gather_v(2, 2, 0, 2 * CHUNK)
         finish_one(1, spill[:])
         nc.sync.dma_start(out=res[high, :T], in_=spill[low, :])
         nc.sync.dma_start(out=res[high, T : 2 * T], in_=spill[high, :])
         nc.sync.dma_start(out=out_flat[:, : 2 * T], in_=res[:, : 2 * T])
+        gather_v(2, 3, 0, 2 * CHUNK)
+        for v0 in (0, 2 * CHUNK):
+            for d in range(2):
+                for t in range(2, PACK):
+                    gather_s(d, t, v0, v0 + 2 * CHUNK)
+        for c in range(2, 4):
+            for t in range(2, PACK):
+                gather_s(2, t, c * CHUNK, (c + 1) * CHUNK)
+        late("hi", "n0", "n1", MAX, 0, 2 * CHUNK)
         late("lo", "n0", "n1", MIN, 0, 2 * CHUNK)
         late("mid", "hi", "n2", MIN, 0, 2 * CHUNK)
+        late("hi", "n0", "n1", MAX, 2 * CHUNK, T)
         finish_late(0, 2 * CHUNK)
         store_late(0, 2 * CHUNK)
-        late("hi", "n0", "n1", MAX, 2 * CHUNK, T)
-        round_to(nc.vector.tensor_copy, 0, 2 * CHUNK)
+        round_to(nc.scalar.copy, 0, 2 * CHUNK)
         late("lo", "n0", "n1", MIN, 2 * CHUNK, T)
-        requantize(0, 2 * CHUNK)
-        store_words(0, 2 * CHUNK)
         late("mid", "hi", "n2", MIN, 2 * CHUNK, 3 * CHUNK)
         late("mid", "hi", "n2", MIN, 3 * CHUNK, T)
         finish_late(2 * CHUNK, 3 * CHUNK)
         round_to(nc.scalar.copy, 2 * CHUNK, 3 * CHUNK)
         finish_late(3 * CHUNK, T)
         store_late(2 * CHUNK, T)
+        requantize(0, 2 * CHUNK)
+        store_words(0, 2 * CHUNK)
         round_to(nc.vector.tensor_copy, 3 * CHUNK, T)
-        requantize(2 * CHUNK, 3 * CHUNK)
         requantize(3 * CHUNK, T)
+        requantize(2 * CHUNK, 3 * CHUNK)
         store_words(2 * CHUNK, T)
 
         for q in range(4):

@@ -98,15 +98,15 @@ def tile_picked_wmedian_none_lo_kernel(tc, x_words, x_scales, w1, pos1, pos2, po
 
         deal(nc.vector.tensor_copy, dealt_a[:], 0, 0, 0, 2)
         deal(nc.vector.tensor_copy, dealt_cd[0][:], 0, 2, 0, 2)
-        for t in range(2):
-            deal(nc.vector.tensor_copy, dealt_a[:, t : t + 1], 0, t, 2, PACK, 1)
+        deal(nc.vector.tensor_copy, dealt_a[:, 0:1], 0, 0, 2, PACK, 1)
+        deal(nc.scalar.copy, dealt_a[:, 1:2], 0, 1, 2, PACK, 1)
         for t in range(2):
             quantize_w(dealt_a[:, t : t + 1], t * HALF, (t + 1) * HALF)
         deal(nc.scalar.copy, dealt_cd[0][:], 0, 2, 2, PACK)
         quantize_cd(0)
-        for c in range(T // CHUNK):
-            project(0, c * CHUNK, (c + 1) * CHUNK)
-            empty(nc.scalar.copy if c % 2 else nc.vector.tensor_copy, 0, c * CHUNK, (c + 1) * CHUNK)
+        for c in range(2):
+            project(0, 2 * c * CHUNK, 2 * (c + 1) * CHUNK)
+            empty(nc.scalar.copy if c % 2 else nc.vector.tensor_copy, 0, 2 * c * CHUNK, 2 * (c + 1) * CHUNK)
 
         res = keep.tile([P, PACK * T], F32, align_bytes=ALIGN)
         res_rows = res[:].rearrange("p (t v) -> p t v", t=PACK)
@@ -136,11 +136,16 @@ def tile_picked_wmedian_none_lo_kernel(tc, x_words, x_scales, w1, pos1, pos2, po
         def gather_v(d, t, v0=0, v1=T):
             nc.vector.tensor_copy(part(f"n{d}", t, v0, v1), looked_up(d, t, v0, v1))
 
-        def one(dst, a, b, op, t):
-            nc.vector.tensor_tensor(part(dst, t, 0, T), part(a, t, 0, T), part(b, t, 0, T), op)
+        def one(dst, a, b, op, t, v0=0, v1=T):
+            nc.vector.tensor_tensor(part(dst, t, v0, v1), part(a, t, v0, v1), part(b, t, v0, v1), op)
 
-        def finish_one(t, dst):
-            nc.vector.tensor_tensor(dst, part("lo", t, 0, T), part("mid", t, 0, T), MAX)
+        def finish(t, dst, v0, v1):
+            middle = (v0 + v1) // 2
+            halves = ((v0, middle), (middle, v1))
+            for h0, h1 in halves:
+                one("mid", "hi", "n2", MIN, t, h0, h1)
+            for h0, h1 in halves:
+                nc.vector.tensor_tensor(dst[:, h0:h1], part("lo", t, h0, h1), part("mid", t, h0, h1), MAX)
 
         def both(kind, v0, v1):
             return work[(1, kind)][:].rearrange("p (t v) -> p t v", t=2)[:, :, v0:v1]
@@ -170,31 +175,28 @@ def tile_picked_wmedian_none_lo_kernel(tc, x_words, x_scales, w1, pos1, pos2, po
         low = slice(0, HALF)
         high = slice(HALF, P)
 
+        for d in range(3):
+            gather_s(d, 0)
         deal(nc.vector.tensor_copy, dealt_b[:], 1, 0)
-        gather_s(0, 0)
-        gather_s(1, 0)
-        deal(nc.vector.tensor_copy, dealt_cd[1][:], 1, 2)
         quantize_w(dealt_b[:], P, 2 * P)
+        deal(nc.vector.tensor_copy, dealt_cd[1][:], 1, 2)
         quantize_cd(1)
         for t in range(1, PACK):
             project(t, 0, T)
-        empty(nc.scalar.copy, 1, 0, T)
-        gather_v(2, 0)
+        empty(nc.vector.tensor_copy, 1, 0, T)
+        gather_v(2, 1)
         for d in range(2):
             gather_s(d, 1)
         for t in range(2, PACK):
-            empty(nc.scalar.copy, t, 0, T)
+            empty(nc.vector.tensor_copy, t, 0, T)
         one("hi", "n0", "n1", MAX, 0)
         one("lo", "n0", "n1", MIN, 0)
-        one("mid", "hi", "n2", MIN, 0)
-        gather_v(2, 1)
-        finish_one(0, res[:, :T])
+        finish(0, res[:, :T], 0, T)
         nc.sync.dma_start(out=res[low, T : 2 * T], in_=res[high, :T])
+        gather_v(2, 2, 0, 2 * CHUNK)
         one("hi", "n0", "n1", MAX, 1)
         one("lo", "n0", "n1", MIN, 1)
-        one("mid", "hi", "n2", MIN, 1)
-        gather_v(2, 2, 0, 2 * CHUNK)
-        finish_one(1, spill[:])
+        finish(1, spill[:], 0, T)
         nc.sync.dma_start(out=res[high, :T], in_=spill[low, :])
         nc.sync.dma_start(out=res[high, T : 2 * T], in_=spill[high, :])
         nc.sync.dma_start(out=out_flat[:, : 2 * T], in_=res[:, : 2 * T])
@@ -208,11 +210,13 @@ def tile_picked_wmedian_none_lo_kernel(tc, x_words, x_scales, w1, pos1, pos2, po
                 gather_s(2, t, c * CHUNK, (c + 1) * CHUNK)
         late("hi", "n0", "n1", MAX, 0, 2 * CHUNK)
         late("lo", "n0", "n1", MIN, 0, 2 * CHUNK)
-        late("mid", "hi", "n2", MIN, 0, 2 * CHUNK)
-        late("hi", "n0", "n1", MAX, 2 * CHUNK, T)
-        finish_late(0, 2 * CHUNK)
+        for t in range(2, PACK):
+            one("mid", "hi", "n2", MIN, t, 0, 2 * CHUNK)
+        for t in range(2, PACK):
+            nc.vector.tensor_tensor(res_rows[:, t, : 2 * CHUNK], part("lo", t, 0, 2 * CHUNK), part("mid", t, 0, 2 * CHUNK), MAX)
         store_late(0, 2 * CHUNK)
         round_to(nc.scalar.copy, 0, 2 * CHUNK)
+        late("hi", "n0", "n1", MAX, 2 * CHUNK, T)
         late("lo", "n0", "n1", MIN, 2 * CHUNK, T)
         late("mid", "hi", "n2", MIN, 2 * CHUNK, 3 * CHUNK)
         late("mid", "hi", "n2", MIN, 3 * CHUNK, T)
@@ -223,8 +227,8 @@ def tile_picked_wmedian_none_lo_kernel(tc, x_words, x_scales, w1, pos1, pos2, po
         requantize(0, 2 * CHUNK)
         store_words(0, 2 * CHUNK)
         round_to(nc.vector.tensor_copy, 3 * CHUNK, T)
-        requantize(3 * CHUNK, T)
         requantize(2 * CHUNK, 3 * CHUNK)
+        requantize(3 * CHUNK, T)
         store_words(2 * CHUNK, T)
 
         for q in range(4):

@@ -62,8 +62,8 @@ def tile_picked_wmedian_none_lo_kernel(tc, x_words, x_scales, w1, pos1, pos2, po
 
         def deal(copy, dst, h, t0, j0=0, j1=PACK, slots=2):
             copy(
-                out=dst.rearrange("p t m j -> p m t j")[:, :, :, j0:j1],
-                in_=w_raw[h][:].rearrange("p j (m t) -> p m t j", t=PACK)[:, :, t0 : t0 + slots, j0:j1],
+                out=dst.rearrange("p t m j -> p m j t")[:, :, j0:j1, :],
+                in_=w_raw[h][:].rearrange("p j (m t) -> p m j t", t=PACK)[:, :, j0:j1, t0 : t0 + slots],
             )
 
         def quantize_w(src, c0, c1):
@@ -160,7 +160,10 @@ def tile_picked_wmedian_none_lo_kernel(tc, x_words, x_scales, w1, pos1, pos2, po
             nc.sync.dma_start(out=out_rows[:, 2:PACK, v0:v1], in_=res_rows[:, 2:PACK, v0:v1])
 
         def round_to(copy, v0, v1):
-            copy(out=rounded[:, v0:v1, :], in_=res_rows[:, :, v0:v1].rearrange("p t v -> p v t"))
+            copy(
+                out=rounded[:, v0:v1, :].rearrange("p (c i) t -> p c t i", i=PACK),
+                in_=res_rows[:, :, v0:v1].rearrange("p t (c i) -> p c t i", i=PACK),
+            )
 
         def requantize(v0, v1):
             nc.vector.quantize_mx(
@@ -175,12 +178,14 @@ def tile_picked_wmedian_none_lo_kernel(tc, x_words, x_scales, w1, pos1, pos2, po
         low = slice(0, HALF)
         high = slice(HALF, P)
 
-        for d in range(3):
-            gather_s(d, 0)
+        gather_s(0, 0)
+        gather_s(2, 0, 2 * CHUNK, T)
+        gather_s(1, 0)
         deal(nc.vector.tensor_copy, dealt_b[:], 1, 0)
-        quantize_w(dealt_b[:], P, 2 * P)
         deal(nc.vector.tensor_copy, dealt_cd[1][:], 1, 2)
+        quantize_w(dealt_b[:], P, 2 * P)
         quantize_cd(1)
+        gather_v(2, 0, 0, 2 * CHUNK)
         for t in range(1, PACK):
             project(t, 0, T)
         empty(nc.vector.tensor_copy, 1, 0, T)
@@ -193,18 +198,20 @@ def tile_picked_wmedian_none_lo_kernel(tc, x_words, x_scales, w1, pos1, pos2, po
         one("lo", "n0", "n1", MIN, 0)
         finish(0, res[:, :T], 0, T)
         nc.sync.dma_start(out=res[low, T : 2 * T], in_=res[high, :T])
-        gather_v(2, 2, 0, 2 * CHUNK)
         one("hi", "n0", "n1", MAX, 1)
         one("lo", "n0", "n1", MIN, 1)
         finish(1, spill[:], 0, T)
         nc.sync.dma_start(out=res[high, :T], in_=spill[low, :])
         nc.sync.dma_start(out=res[high, T : 2 * T], in_=spill[high, :])
         nc.sync.dma_start(out=out_flat[:, : 2 * T], in_=res[:, : 2 * T])
-        gather_v(2, 3, 0, 2 * CHUNK)
-        for v0 in (0, 2 * CHUNK):
-            for d in range(2):
-                for t in range(2, PACK):
-                    gather_s(d, t, v0, v0 + 2 * CHUNK)
+        gather_v(2, 2, 0, 2 * CHUNK)
+        for d in range(2):
+            for t in range(2, PACK):
+                gather_s(d, t, 0, 2 * CHUNK)
+        gather_s(2, 3, 0, 2 * CHUNK)
+        for d in range(2):
+            for t in range(2, PACK):
+                gather_s(d, t, 2 * CHUNK, T)
         for c in range(2, 4):
             for t in range(2, PACK):
                 gather_s(2, t, c * CHUNK, (c + 1) * CHUNK)

@@ -54,6 +54,8 @@ def tile_picked_wmedian_none_lo_kernel(tc, x_words, x_scales, w1, pos1, pos2, po
 
         y = [keep.tile([P, T + SPARE], F32, align_bytes=ALIGN, name=f"y{t}") for t in range(PACK)]
 
+        nc.vector.memset(y[0][:, T:], 0.0)
+
         dealt_a = keep.tile([P, 2, HALF, PACK], BF16, align_bytes=ALIGN)
         dealt_b = keep.tile([P, 2, HALF, PACK], BF16, align_bytes=ALIGN)
         dealt_cd = [keep.tile([P, 2, HALF, PACK], BF16, align_bytes=ALIGN, name=f"dealt_cd{h}") for h in range(2)]

@@ -181,13 +181,13 @@ def tile_picked_wmedian_none_lo_kernel(tc, x_words, x_scales, w1, pos1, pos2, po
         high = slice(HALF, P)
 
         gather_s(0, 0)
-        gather_s(2, 0, 2 * CHUNK, T)
+        gather_s(2, 0, 3 * CHUNK, T)
         gather_s(1, 0)
         deal(nc.vector.tensor_copy, dealt_b[:], 1, 0)
         deal(nc.vector.tensor_copy, dealt_cd[1][:], 1, 2)
         quantize_w(dealt_b[:], P, 2 * P)
         quantize_cd(1)
-        gather_v(2, 0, 0, 2 * CHUNK)
+        gather_v(2, 0, 0, 3 * CHUNK)
         for t in range(1, PACK):
             project(t, 0, T)
         empty(nc.vector.tensor_copy, 1, 0, T)
@@ -205,12 +205,11 @@ def tile_picked_wmedian_none_lo_kernel(tc, x_words, x_scales, w1, pos1, pos2, po
         finish(1, spill[:], 0, T)
         nc.sync.dma_start(out=res[high, :T], in_=spill[low, :])
         nc.sync.dma_start(out=res[high, T : 2 * T], in_=spill[high, :])
-        nc.sync.dma_start(out=out_flat[:, : 2 * T], in_=res[:, : 2 * T])
-        gather_v(2, 2, 0, 2 * CHUNK)
         for d in range(2):
             for t in range(2, PACK):
                 gather_s(d, t, 0, 2 * CHUNK)
-        gather_s(2, 3, 0, 2 * CHUNK)
+        for t in range(2, PACK):
+            gather_s(2, t, 0, 2 * CHUNK)
         for d in range(2):
             for t in range(2, PACK):
                 gather_s(d, t, 2 * CHUNK, T)
@@ -224,6 +223,7 @@ def tile_picked_wmedian_none_lo_kernel(tc, x_words, x_scales, w1, pos1, pos2, po
         for t in range(2, PACK):
             nc.vector.tensor_tensor(res_rows[:, t, : 2 * CHUNK], part("lo", t, 0, 2 * CHUNK), part("mid", t, 0, 2 * CHUNK), MAX)
         store_late(0, 2 * CHUNK)
+        nc.sync.dma_start(out=out_flat[:, : 2 * T], in_=res[:, : 2 * T])
         round_to(nc.scalar.copy, 0, 2 * CHUNK)
         late("hi", "n0", "n1", MAX, 2 * CHUNK, T)
         late("lo", "n0", "n1", MIN, 2 * CHUNK, T)

@@ -25,6 +25,7 @@ QUADRANT = 32
 LIST_ROWS = 16
 SPARE = 192
 CHUNK = 128
+SHARE = 416
 
 
 def tile_picked_wmedian_none_lo_kernel(tc, x_words, x_scales, w1, pos1, pos2, pos3, out_0, out_1, out_2):
@@ -181,13 +182,13 @@ def tile_picked_wmedian_none_lo_kernel(tc, x_words, x_scales, w1, pos1, pos2, po
         high = slice(HALF, P)
 
         gather_s(0, 0)
-        gather_s(2, 0, 3 * CHUNK, T)
+        gather_s(2, 0, SHARE, T)
         gather_s(1, 0)
         deal(nc.vector.tensor_copy, dealt_b[:], 1, 0)
         deal(nc.vector.tensor_copy, dealt_cd[1][:], 1, 2)
         quantize_w(dealt_b[:], P, 2 * P)
+        gather_v(2, 0, 0, SHARE)
         quantize_cd(1)
-        gather_v(2, 0, 0, 3 * CHUNK)
         for t in range(1, PACK):
             project(t, 0, T)
         empty(nc.vector.tensor_copy, 1, 0, T)
@@ -206,16 +207,15 @@ def tile_picked_wmedian_none_lo_kernel(tc, x_words, x_scales, w1, pos1, pos2, po
         nc.sync.dma_start(out=res[high, :T], in_=spill[low, :])
         nc.sync.dma_start(out=res[high, T : 2 * T], in_=spill[high, :])
         for d in range(2):
-            for t in range(2, PACK):
-                gather_s(d, t, 0, 2 * CHUNK)
+            gather_s(d, 2)
+            gather_s(d, 3, 0, 2 * CHUNK)
         for t in range(2, PACK):
             gather_s(2, t, 0, 2 * CHUNK)
         for d in range(2):
-            for t in range(2, PACK):
-                gather_s(d, t, 2 * CHUNK, T)
+            gather_s(d, 3, 2 * CHUNK, T)
+        gather_s(2, 2, 2 * CHUNK, T)
         for c in range(2, 4):
-            for t in range(2, PACK):
-                gather_s(2, t, c * CHUNK, (c + 1) * CHUNK)
+            gather_s(2, 3, c * CHUNK, (c + 1) * CHUNK)
         late("hi", "n0", "n1", MAX, 0, 2 * CHUNK)
         late("lo", "n0", "n1", MIN, 0, 2 * CHUNK)
         for t in range(2, PACK):

@@ -25,7 +25,7 @@ QUADRANT = 32
 LIST_ROWS = 16
 SPARE = 192
 CHUNK = 128
-SHARE = 416
+SHARE = 384
 
 
 def tile_picked_wmedian_none_lo_kernel(tc, x_words, x_scales, w1, pos1, pos2, pos3, out_0, out_1, out_2):

@@ -42,12 +42,12 @@ def tile_picked_wmedian_none_lo_kernel(tc, x_words, x_scales, w1, pos1, pos2, po
 
         for u in range(2):
             nc.sync.dma_start(out=w_raw[0][:, 2 * u : 2 * u + 2, :], in_=w_rows[:, 2 * u : 2 * u + 2, : N // 2])
+        nc.sync.dma_start(out=x_codes[:].bitcast(I32), in_=x_words[0].bitcast(I32))
         for q in range(4):
-            nc.sync.dma_start(
+            (nc.scalar if q < 2 else nc.sync).dma_start(
                 out=x_planes[QUADRANT * q : QUADRANT * q + 4, :].bitcast(I32),
                 in_=x_scales[0, 4 * q : 4 * q + 4, :].bitcast(I32),
             )
-        nc.sync.dma_start(out=x_codes[:].bitcast(I32), in_=x_words[0].bitcast(I32))
         nc.sync.dma_start(out=w_raw[1][:], in_=w_rows[:, :, N // 2 :])
         nc.sync.dma_start(lists[0][:], pos1)
         nc.sync.dma_start(lists[1][:], pos2)

@@ -25,7 +25,7 @@ QUADRANT = 32
 LIST_ROWS = 16
 SPARE = 192
 CHUNK = 128
-SHARE = 384
+CUT = 44
 
 
 def tile_picked_wmedian_none_lo_kernel(tc, x_words, x_scales, w1, pos1, pos2, pos3, out_0, out_1, out_2):
@@ -40,18 +40,18 @@ def tile_picked_wmedian_none_lo_kernel(tc, x_words, x_scales, w1, pos1, pos2, po
         x_codes = keep.tile([P, 2 * T], U8, align_bytes=ALIGN)
         x_planes = keep.tile([P, T], U8, align_bytes=ALIGN)
 
-        for u in range(2):
-            nc.sync.dma_start(out=w_raw[0][:, 2 * u : 2 * u + 2, :], in_=w_rows[:, 2 * u : 2 * u + 2, : N // 2])
-        nc.sync.dma_start(out=x_codes[:].bitcast(I32), in_=x_words[0].bitcast(I32))
+        nc.sync.dma_start(lists[0][:], pos1)
+        nc.sync.dma_start(out=w_raw[0][:], in_=w_rows[:, :, : N // 2])
         for q in range(4):
-            (nc.scalar if q < 2 else nc.sync).dma_start(
+            nc.sync.dma_start(
                 out=x_planes[QUADRANT * q : QUADRANT * q + 4, :].bitcast(I32),
                 in_=x_scales[0, 4 * q : 4 * q + 4, :].bitcast(I32),
             )
-        nc.sync.dma_start(out=w_raw[1][:], in_=w_rows[:, :, N // 2 :])
-        nc.sync.dma_start(lists[0][:], pos1)
-        nc.sync.dma_start(lists[1][:], pos2)
+        nc.sync.dma_start(out=x_codes[:].bitcast(I32), in_=x_words[0].bitcast(I32))
+        for u in range(2):
+            nc.sync.dma_start(out=w_raw[1][:, 2 * u : 2 * u + 2, :], in_=w_rows[:, 2 * u : 2 * u + 2, N // 2 :])
         nc.sync.dma_start(lists[2][:], pos3)
+        nc.sync.dma_start(lists[1][:], pos2)
 
         y = [keep.tile([P, T + SPARE], F32, align_bytes=ALIGN, name=f"y{t}") for t in range(PACK)]
 
@@ -63,10 +63,10 @@ def tile_picked_wmedian_none_lo_kernel(tc, x_words, x_scales, w1, pos1, pos2, po
         w_codes = keep.tile([P, N], U32, align_bytes=ALIGN)
         w_planes = keep.tile([P, N], U8, align_bytes=ALIGN)
 
-        def deal(copy, dst, h, t0, j0=0, j1=PACK, slots=2):
+        def deal(copy, dst, h, t0, j0=0, j1=PACK, slots=2, m0=0, m1=HALF):
             copy(
                 out=dst.rearrange("p t m j -> p m j t")[:, :, j0:j1, :],
-                in_=w_raw[h][:].rearrange("p j (m t) -> p m j t", t=PACK)[:, :, j0:j1, t0 : t0 + slots],
+                in_=w_raw[h][:].rearrange("p j (m t) -> p m j t", t=PACK)[:, m0:m1, j0:j1, t0 : t0 + slots],
             )
 
         def quantize_w(src, c0, c1):
@@ -99,17 +99,16 @@ def tile_picked_wmedian_none_lo_kernel(tc, x_words, x_scales, w1, pos1, pos2, po
         def empty(copy, t, c0, c1):
             copy(out=y[t][:, c0:c1], in_=banks[(t, c0)][:])
 
-        deal(nc.vector.tensor_copy, dealt_a[:], 0, 0, 0, 2)
-        deal(nc.vector.tensor_copy, dealt_cd[0][:], 0, 2, 0, 2)
-        deal(nc.vector.tensor_copy, dealt_a[:, 0:1], 0, 0, 2, PACK, 1)
-        deal(nc.scalar.copy, dealt_a[:, 1:2], 0, 1, 2, PACK, 1)
-        for t in range(2):
-            quantize_w(dealt_a[:, t : t + 1], t * HALF, (t + 1) * HALF)
-        deal(nc.scalar.copy, dealt_cd[0][:], 0, 2, 2, PACK)
+        deal(nc.vector.tensor_copy, dealt_a[:, :, :CUT], 0, 0, m1=CUT)
+        deal(nc.scalar.copy, dealt_a[:, :, CUT:], 0, 0, m0=CUT)
+        quantize_w(dealt_a[:], 0, P)
+        deal(nc.scalar.copy, dealt_cd[0][:], 0, 2)
         quantize_cd(0)
+        deal(nc.vector.tensor_copy, dealt_b[:], 1, 0, 0, 2)
+        deal(nc.vector.tensor_copy, dealt_cd[1][:], 1, 2, 0, 2)
         for c in range(2):
             project(0, 2 * c * CHUNK, 2 * (c + 1) * CHUNK)
-            empty(nc.scalar.copy if c % 2 else nc.vector.tensor_copy, 0, 2 * c * CHUNK, 2 * (c + 1) * CHUNK)
+            empty(nc.scalar.copy, 0, 2 * c * CHUNK, 2 * (c + 1) * CHUNK)
 
         res = keep.tile([P, PACK * T], F32, align_bytes=ALIGN)
         res_rows = res[:].rearrange("p (t v) -> p t v", t=PACK)
@@ -182,12 +181,11 @@ def tile_picked_wmedian_none_lo_kernel(tc, x_words, x_scales, w1, pos1, pos2, po
         high = slice(HALF, P)
 
         gather_s(0, 0)
-        gather_s(2, 0, SHARE, T)
         gather_s(1, 0)
-        deal(nc.vector.tensor_copy, dealt_b[:], 1, 0)
-        deal(nc.vector.tensor_copy, dealt_cd[1][:], 1, 2)
+        deal(nc.vector.tensor_copy, dealt_b[:], 1, 0, 2, PACK)
+        deal(nc.vector.tensor_copy, dealt_cd[1][:], 1, 2, 2, PACK)
         quantize_w(dealt_b[:], P, 2 * P)
-        gather_v(2, 0, 0, SHARE)
+        gather_v(2, 0)
         quantize_cd(1)
         for t in range(1, PACK):
             project(t, 0, T)

@@ -122,9 +122,11 @@ def tile_picked_wmedian_none_lo_kernel(tc, x_words, x_scales, w1, pos1, pos2, po
 
         work = {}
         for step in range(2):
-            for kind in ("n0", "n1", "n2", "hi", "lo", "mid"):
+            for kind in ("n0", "n1", "hi", "lo", "mid") + (("n2",) if step == 0 else ()):
                 whole = keep.tile([P, 2 * T], F32, align_bytes=ALIGN, name=f"{kind}{step}")
                 work[(step, kind)] = whole
+
+        work[(1, "n2")] = work[(0, "mid")]
 
         def part(kind, t, v0, v1):
             return work[(t // 2, kind)][:, (t % 2) * T + v0 : (t % 2) * T + v1]
@@ -189,12 +191,10 @@ def tile_picked_wmedian_none_lo_kernel(tc, x_words, x_scales, w1, pos1, pos2, po
         quantize_cd(1)
         for t in range(1, PACK):
             project(t, 0, T)
-        empty(nc.vector.tensor_copy, 1, 0, T)
-        gather_v(2, 1)
-        for d in range(2):
-            gather_s(d, 1)
-        for t in range(2, PACK):
+        for t in range(1, PACK):
             empty(nc.vector.tensor_copy, t, 0, T)
+        for d in range(3):
+            gather_s(d, 1)
         one("hi", "n0", "n1", MAX, 0)
         one("lo", "n0", "n1", MIN, 0)
         finish(0, res[:, :T], 0, T)
@@ -204,13 +204,12 @@ def tile_picked_wmedian_none_lo_kernel(tc, x_words, x_scales, w1, pos1, pos2, po
         finish(1, spill[:], 0, T)
         nc.sync.dma_start(out=res[high, :T], in_=spill[low, :])
         nc.sync.dma_start(out=res[high, T : 2 * T], in_=spill[high, :])
-        for d in range(2):
-            gather_s(d, 2)
-            gather_s(d, 3, 0, 2 * CHUNK)
         for t in range(2, PACK):
-            gather_s(2, t, 0, 2 * CHUNK)
-        for d in range(2):
-            gather_s(d, 3, 2 * CHUNK, T)
+            gather_v(2, t, 0, 2 * CHUNK)
+        for v0 in (0, 2 * CHUNK):
+            for d in range(2):
+                for t in range(2, PACK):
+                    gather_s(d, t, v0, v0 + 2 * CHUNK)
         gather_s(2, 2, 2 * CHUNK, T)
         for c in range(2, 4):
             gather_s(2, 3, c * CHUNK, (c + 1) * CHUNK)

@@ -25,7 +25,6 @@ QUADRANT = 32
 LIST_ROWS = 16
 SPARE = 192
 CHUNK = 128
-CUT = 44
 
 
 def tile_picked_wmedian_none_lo_kernel(tc, x_words, x_scales, w1, pos1, pos2, pos3, out_0, out_1, out_2):
@@ -35,12 +34,12 @@ def tile_picked_wmedian_none_lo_kernel(tc, x_words, x_scales, w1, pos1, pos2, po
         psum = ctx.enter_context(tc.psum_pool(name="psum", bufs=1))
 
         w_rows = w1.rearrange("(p j) c -> p j c", j=PACK)
-        w_raw = [keep.tile([P, PACK, N // 2], F32, align_bytes=ALIGN, name=f"w_raw{h}") for h in range(2)]
+        w_raw = [keep.tile([P, PACK, N // 2], F32, align_bytes=ALIGN, name=f"w_raw{h}", tag=f"w_raw{h}") for h in range(2)]
         lists = [keep.tile([P, T // LIST_ROWS], U16, name=f"offsets{d}") for d in range(3)]
         x_codes = keep.tile([P, 2 * T], U8, align_bytes=ALIGN)
         x_planes = keep.tile([P, T], U8, align_bytes=ALIGN)
 
-        nc.sync.dma_start(lists[0][:], pos1)
+        nc.sync.dma_start(lists[2][:], pos3)
         nc.sync.dma_start(out=w_raw[0][:], in_=w_rows[:, :, : N // 2])
         for q in range(4):
             nc.sync.dma_start(
@@ -50,7 +49,7 @@ def tile_picked_wmedian_none_lo_kernel(tc, x_words, x_scales, w1, pos1, pos2, po
         nc.sync.dma_start(out=x_codes[:].bitcast(I32), in_=x_words[0].bitcast(I32))
         for u in range(2):
             nc.sync.dma_start(out=w_raw[1][:, 2 * u : 2 * u + 2, :], in_=w_rows[:, 2 * u : 2 * u + 2, N // 2 :])
-        nc.sync.dma_start(lists[2][:], pos3)
+        nc.sync.dma_start(lists[0][:], pos1)
         nc.sync.dma_start(lists[1][:], pos2)
 
         y = [keep.tile([P, T + SPARE], F32, align_bytes=ALIGN, name=f"y{t}") for t in range(PACK)]
@@ -99,8 +98,7 @@ def tile_picked_wmedian_none_lo_kernel(tc, x_words, x_scales, w1, pos1, pos2, po
         def empty(copy, t, c0, c1):
             copy(out=y[t][:, c0:c1], in_=banks[(t, c0)][:])
 
-        deal(nc.vector.tensor_copy, dealt_a[:, :, :CUT], 0, 0, m1=CUT)
-        deal(nc.scalar.copy, dealt_a[:, :, CUT:], 0, 0, m0=CUT)
+        deal(nc.vector.tensor_copy, dealt_a[:], 0, 0)
         quantize_w(dealt_a[:], 0, P)
         deal(nc.scalar.copy, dealt_cd[0][:], 0, 2)
         quantize_cd(0)
@@ -109,6 +107,11 @@ def tile_picked_wmedian_none_lo_kernel(tc, x_words, x_scales, w1, pos1, pos2, po
         for c in range(2):
             project(0, 2 * c * CHUNK, 2 * (c + 1) * CHUNK)
             empty(nc.scalar.copy, 0, 2 * c * CHUNK, 2 * (c + 1) * CHUNK)
+
+        deal(nc.vector.tensor_copy, dealt_b[:], 1, 0, 2, PACK)
+        deal(nc.vector.tensor_copy, dealt_cd[1][:], 1, 2, 2, PACK)
+        quantize_w(dealt_b[:], P, 2 * P)
+        quantize_cd(1)
 
         res = keep.tile([P, PACK * T], F32, align_bytes=ALIGN)
         res_rows = res[:].rearrange("p (t v) -> p t v", t=PACK)
@@ -123,7 +126,8 @@ def tile_picked_wmedian_none_lo_kernel(tc, x_words, x_scales, w1, pos1, pos2, po
         work = {}
         for step in range(2):
             for kind in ("n0", "n1", "hi", "lo", "mid") + (("n2",) if step == 0 else ()):
-                whole = keep.tile([P, 2 * T], F32, align_bytes=ALIGN, name=f"{kind}{step}")
+                tag = "w_raw1" if kind == "n2" else f"{kind}{step}"
+                whole = keep.tile([P, 2 * T], F32, align_bytes=ALIGN, name=f"{kind}{step}", tag=tag)
                 work[(step, kind)] = whole
 
         work[(1, "n2")] = work[(0, "mid")]
@@ -184,11 +188,7 @@ def tile_picked_wmedian_none_lo_kernel(tc, x_words, x_scales, w1, pos1, pos2, po
 
         gather_s(0, 0)
         gather_s(1, 0)
-        deal(nc.vector.tensor_copy, dealt_b[:], 1, 0, 2, PACK)
-        deal(nc.vector.tensor_copy, dealt_cd[1][:], 1, 2, 2, PACK)
-        quantize_w(dealt_b[:], P, 2 * P)
         gather_v(2, 0)
-        quantize_cd(1)
         for t in range(1, PACK):
             project(t, 0, T)
         for t in range(1, PACK):

@@ -25,6 +25,8 @@ QUADRANT = 32
 LIST_ROWS = 16
 SPARE = 192
 CHUNK = 128
+CUT = 44
+SHARE = 64
 
 
 def tile_picked_wmedian_none_lo_kernel(tc, x_words, x_scales, w1, pos1, pos2, pos3, out_0, out_1, out_2):
@@ -98,7 +100,8 @@ def tile_picked_wmedian_none_lo_kernel(tc, x_words, x_scales, w1, pos1, pos2, po
         def empty(copy, t, c0, c1):
             copy(out=y[t][:, c0:c1], in_=banks[(t, c0)][:])
 
-        deal(nc.vector.tensor_copy, dealt_a[:], 0, 0)
+        deal(nc.vector.tensor_copy, dealt_a[:, :, :CUT], 0, 0, m1=CUT)
+        deal(nc.scalar.copy, dealt_a[:, :, CUT:], 0, 0, m0=CUT)
         quantize_w(dealt_a[:], 0, P)
         deal(nc.scalar.copy, dealt_cd[0][:], 0, 2)
         quantize_cd(0)
@@ -193,8 +196,10 @@ def tile_picked_wmedian_none_lo_kernel(tc, x_words, x_scales, w1, pos1, pos2, po
             project(t, 0, T)
         for t in range(1, PACK):
             empty(nc.vector.tensor_copy, t, 0, T)
-        for d in range(3):
+        gather_v(2, 1, 0, SHARE)
+        for d in range(2):
             gather_s(d, 1)
+        gather_s(2, 1, SHARE, T)
         one("hi", "n0", "n1", MAX, 0)
         one("lo", "n0", "n1", MIN, 0)
         finish(0, res[:, :T], 0, T)
@@ -227,9 +232,10 @@ def tile_picked_wmedian_none_lo_kernel(tc, x_words, x_scales, w1, pos1, pos2, po
         late("mid", "hi", "n2", MIN, 2 * CHUNK, 3 * CHUNK)
         late("mid", "hi", "n2", MIN, 3 * CHUNK, T)
         finish_late(2 * CHUNK, 3 * CHUNK)
+        store_late(2 * CHUNK, 3 * CHUNK)
         round_to(nc.scalar.copy, 2 * CHUNK, 3 * CHUNK)
         finish_late(3 * CHUNK, T)
-        store_late(2 * CHUNK, T)
+        store_late(3 * CHUNK, T)
         requantize(0, 2 * CHUNK)
         store_words(0, 2 * CHUNK)
         round_to(nc.vector.tensor_copy, 3 * CHUNK, T)

from contextlib import ExitStack

import concourse.mybir as mybir

K, T, N = 512, 512, 512
FLOPS = 2 * K * T * N

F32 = mybir.dt.float32
BF16 = mybir.dt.bfloat16
I32 = mybir.dt.int32
U32 = mybir.dt.uint32
U16 = mybir.dt.uint16
U8 = mybir.dt.uint8
FP8X4 = mybir.dt.float8_e4m3fn_x4
FP4X4 = mybir.dt.float4_e2m1fn_x4
MIN = mybir.AluOpType.min
MAX = mybir.AluOpType.max
COPY = mybir.ActivationFunctionType.Copy

P = 128
ALIGN = 256
PACK = 4
HALF = P // 2
QUADRANT = 32
LIST_ROWS = 16
SPARE = 192
CHUNK = 128
CUT = 44
SHARE = 64


def tile_picked_wmedian_none_lo_kernel(tc, x_words, x_scales, w1, pos1, pos2, pos3, out_0, out_1, out_2):
    nc = tc.nc
    with ExitStack() as ctx:
        keep = ctx.enter_context(tc.tile_pool(name="keep", bufs=1))
        psum = ctx.enter_context(tc.psum_pool(name="psum", bufs=1))

        w_rows = w1.rearrange("(p j) c -> p j c", j=PACK)
        w_raw = [keep.tile([P, PACK, N // 2], F32, align_bytes=ALIGN, name=f"w_raw{h}", tag=f"w_raw{h}") for h in range(2)]
        lists = [keep.tile([P, T // LIST_ROWS], U16, name=f"offsets{d}") for d in range(3)]
        x_codes = keep.tile([P, 2 * T], U8, align_bytes=ALIGN)
        x_planes = keep.tile([P, T], U8, align_bytes=ALIGN)

        nc.sync.dma_start(lists[2][:], pos3)
        nc.sync.dma_start(out=w_raw[0][:], in_=w_rows[:, :, : N // 2])
        for q in range(4):
            nc.sync.dma_start(
                out=x_planes[QUADRANT * q : QUADRANT * q + 4, :].bitcast(I32),
                in_=x_scales[0, 4 * q : 4 * q + 4, :].bitcast(I32),
            )
        nc.sync.dma_start(out=x_codes[:].bitcast(I32), in_=x_words[0].bitcast(I32))
        for u in range(2):
            nc.sync.dma_start(out=w_raw[1][:, 2 * u : 2 * u + 2, :], in_=w_rows[:, 2 * u : 2 * u + 2, N // 2 :])
        nc.sync.dma_start(lists[0][:], pos1)
        nc.sync.dma_start(lists[1][:], pos2)

        y = [keep.tile([P, T + SPARE], F32, align_bytes=ALIGN, name=f"y{t}") for t in range(PACK)]

        nc.vector.memset(y[0][:, T:], 0.0)

        dealt_a = keep.tile([P, 2, HALF, PACK], BF16, align_bytes=ALIGN)
        dealt_b = keep.tile([P, 2, HALF, PACK], BF16, align_bytes=ALIGN)
        dealt_cd = [keep.tile([P, 2, HALF, PACK], BF16, align_bytes=ALIGN, name=f"dealt_cd{h}") for h in range(2)]
        w_codes = keep.tile([P, N], U32, align_bytes=ALIGN)
        w_planes = keep.tile([P, N], U8, align_bytes=ALIGN)

        def deal(copy, dst, h, t0, j0=0, j1=PACK, slots=2, m0=0, m1=HALF):
            copy(
                out=dst.rearrange("p t m j -> p m j t")[:, :, j0:j1, :],
                in_=w_raw[h][:].rearrange("p j (m t) -> p m j t", t=PACK)[:, m0:m1, j0:j1, t0 : t0 + slots],
            )

        def quantize_w(src, c0, c1):
            nc.vector.quantize_mx(
                out=w_codes[:, c0:c1].bitcast(FP8X4),
                scales=w_planes[:, c0:c1],
                in_=src.rearrange("p t m j -> p (t m j)"),
            )

        def quantize_cd(h):
            for t in range(2):
                c0 = (2 + t) * P + h * HALF
                quantize_w(dealt_cd[h][:, t : t + 1], c0, c0 + HALF)

        banks = {}

        def project(t, c0, c1):
            bank = psum.tile([P, c1 - c0], F32, name=f"bank{t}_{c0}")
            nc.tensor.matmul_mx(
                out=bank[:],
                lhsT=w_codes[:, t * P : (t + 1) * P].bitcast(FP8X4),
                lhsT_scale=w_planes[:, t * P : (t + 1) * P],
                rhs=x_codes[:, 2 * c0 : 2 * c1].bitcast(FP4X4),
                rhs_scale=x_planes[:, c0:c1],
                start=True,
                stop=True,
            )
            banks[(t, c0)] = bank

        def empty(copy, t, c0, c1):
            copy(out=y[t][:, c0:c1], in_=banks[(t, c0)][:])

        deal(nc.vector.tensor_copy, dealt_a[:, :, :CUT], 0, 0, m1=CUT)
        deal(nc.scalar.copy, dealt_a[:, :, CUT:], 0, 0, m0=CUT)
        quantize_w(dealt_a[:], 0, P)
        deal(nc.scalar.copy, dealt_cd[0][:], 0, 2)
        quantize_cd(0)
        deal(nc.vector.tensor_copy, dealt_b[:], 1, 0, 0, 2)
        deal(nc.vector.tensor_copy, dealt_cd[1][:], 1, 2, 0, 2)
        for c in range(2):
            project(0, 2 * c * CHUNK, 2 * (c + 1) * CHUNK)
            empty(nc.scalar.copy, 0, 2 * c * CHUNK, 2 * (c + 1) * CHUNK)

        deal(nc.vector.tensor_copy, dealt_b[:], 1, 0, 2, PACK)
        deal(nc.vector.tensor_copy, dealt_cd[1][:], 1, 2, 2, PACK)
        quantize_w(dealt_b[:], P, 2 * P)
        quantize_cd(1)

        res = keep.tile([P, PACK * T], F32, align_bytes=ALIGN)
        res_rows = res[:].rearrange("p (t v) -> p t v", t=PACK)
        spill = keep.tile([P, T], F32, align_bytes=ALIGN)
        rounded = keep.tile([P, T, PACK], BF16, align_bytes=ALIGN)
        o_codes = keep.tile([P, T], U32, align_bytes=ALIGN)
        o_planes = keep.tile([P, T], U8, align_bytes=ALIGN)
        out_flat = out_0.rearrange("(p t) v -> p (t v)", t=PACK)
        out_rows = out_0.rearrange("(p t) v -> p t v", t=PACK)
        out_words = out_1[0].rearrange("p v t -> p (v t)").bitcast(I32)

        work = {}
        for step in range(2):
            for kind in ("n0", "n1", "hi", "lo", "mid") + (("n2",) if step == 0 else ()):
                tag = "w_raw1" if kind == "n2" else f"{kind}{step}"
                whole = keep.tile([P, 2 * T], F32, align_bytes=ALIGN, name=f"{kind}{step}", tag=tag)
                work[(step, kind)] = whole

        work[(1, "n2")] = work[(0, "mid")]

        def part(kind, t, v0, v1):
            return work[(t // 2, kind)][:, (t % 2) * T + v0 : (t % 2) * T + v1]

        def looked_up(d, t, v0, v1):
            return y[t][:].indirect(lists[d][:, v0 // LIST_ROWS : v1 // LIST_ROWS])

        def gather_s(d, t, v0=0, v1=T):
            nc.scalar.activation(part(f"n{d}", t, v0, v1), looked_up(d, t, v0, v1), COPY)

        def gather_v(d, t, v0=0, v1=T):
            nc.vector.tensor_copy(part(f"n{d}", t, v0, v1), looked_up(d, t, v0, v1))

        def one(dst, a, b, op, t, v0=0, v1=T):
            nc.vector.tensor_tensor(part(dst, t, v0, v1), part(a, t, v0, v1), part(b, t, v0, v1), op)

        def finish(t, dst, v0, v1):
            middle = (v0 + v1) // 2
            halves = ((v0, middle), (middle, v1))
            for h0, h1 in halves:
                one("mid", "hi", "n2", MIN, t, h0, h1)
            for h0, h1 in halves:
                nc.vector.tensor_tensor(dst[:, h0:h1], part("lo", t, h0, h1), part("mid", t, h0, h1), MAX)

        def both(kind, v0, v1):
            return work[(1, kind)][:].rearrange("p (t v) -> p t v", t=2)[:, :, v0:v1]

        def late(dst, a, b, op, v0, v1):
            nc.vector.tensor_tensor(both(dst, v0, v1), both(a, v0, v1), both(b, v0, v1), op)

        def finish_late(v0, v1):
            nc.vector.tensor_tensor(res_rows[:, 2:PACK, v0:v1], both("lo", v0, v1), both("mid", v0, v1), MAX)

        def store_late(v0, v1):
            nc.sync.dma_start(out=out_rows[:, 2:PACK, v0:v1], in_=res_rows[:, 2:PACK, v0:v1])

        def round_to(copy, v0, v1):
            copy(
                out=rounded[:, v0:v1, :].rearrange("p (c i) t -> p c t i", i=PACK),
                in_=res_rows[:, :, v0:v1].rearrange("p t (c i) -> p c t i", i=PACK),
            )

        def requantize(v0, v1):
            nc.vector.quantize_mx(
                out=o_codes[:, v0:v1].bitcast(FP8X4),
                scales=o_planes[:, v0:v1],
                in_=rounded[:, v0:v1, :].rearrange("p v t -> p (v t)"),
            )

        def store_words(v0, v1):
            nc.sync.dma_start(out=out_words[:, v0:v1], in_=o_codes[:, v0:v1].bitcast(I32))

        low = slice(0, HALF)
        high = slice(HALF, P)

        gather_s(0, 0)
        gather_s(1, 0)
        gather_v(2, 0)
        for t in range(1, PACK):
            project(t, 0, T)
        for t in range(1, PACK):
            empty(nc.vector.tensor_copy, t, 0, T)
        gather_v(2, 1, 0, SHARE)
        for d in range(2):
            gather_s(d, 1)
        gather_s(2, 1, SHARE, T)
        one("hi", "n0", "n1", MAX, 0)
        one("lo", "n0", "n1", MIN, 0)
        finish(0, res[:, :T], 0, T)
        nc.sync.dma_start(out=res[low, T : 2 * T], in_=res[high, :T])
        one("hi", "n0", "n1", MAX, 1)
        one("lo", "n0", "n1", MIN, 1)
        finish(1, spill[:], 0, T)
        nc.sync.dma_start(out=res[high, :T], in_=spill[low, :])
        nc.sync.dma_start(out=res[high, T : 2 * T], in_=spill[high, :])
        for t in range(2, PACK):
            gather_v(2, t, 0, 2 * CHUNK)
        for v0 in (0, 2 * CHUNK):
            for d in range(2):
                for t in range(2, PACK):
                    gather_s(d, t, v0, v0 + 2 * CHUNK)
        gather_s(2, 2, 2 * CHUNK, T)
        for c in range(2, 4):
            gather_s(2, 3, c * CHUNK, (c + 1) * CHUNK)
        late("hi", "n0", "n1", MAX, 0, 2 * CHUNK)
        late("lo", "n0", "n1", MIN, 0, 2 * CHUNK)
        for t in range(2, PACK):
            one("mid", "hi", "n2", MIN, t, 0, 2 * CHUNK)
        for t in range(2, PACK):
            nc.vector.tensor_tensor(res_rows[:, t, : 2 * CHUNK], part("lo", t, 0, 2 * CHUNK), part("mid", t, 0, 2 * CHUNK), MAX)
        store_late(0, 2 * CHUNK)
        nc.sync.dma_start(out=out_flat[:, : 2 * T], in_=res[:, : 2 * T])
        round_to(nc.scalar.copy, 0, 2 * CHUNK)
        late("hi", "n0", "n1", MAX, 2 * CHUNK, T)
        late("lo", "n0", "n1", MIN, 2 * CHUNK, T)
        late("mid", "hi", "n2", MIN, 2 * CHUNK, 3 * CHUNK)
        late("mid", "hi", "n2", MIN, 3 * CHUNK, T)
        finish_late(2 * CHUNK, 3 * CHUNK)
        store_late(2 * CHUNK, 3 * CHUNK)
        round_to(nc.scalar.copy, 2 * CHUNK, 3 * CHUNK)
        finish_late(3 * CHUNK, T)
        store_late(3 * CHUNK, T)
        requantize(0, 2 * CHUNK)
        store_words(0, 2 * CHUNK)
        round_to(nc.vector.tensor_copy, 3 * CHUNK, T)
        requantize(2 * CHUNK, 3 * CHUNK)
        requantize(3 * CHUNK, T)
        store_words(2 * CHUNK, T)

        for q in range(4):
            queue = nc.scalar if q == 0 else nc.sync
            queue.dma_start(
                out=out_2[0, 4 * q : 4 * q + 4, :].bitcast(I32),
                in_=o_planes[QUADRANT * q : QUADRANT * q + 4, :].bitcast(I32),
            )
